import numpy as np
import ml_dtypes


def mxq(x, axis, fmt="e4m3"):
    dtype, down = {"e4m3": (ml_dtypes.float8_e4m3fn, 7), "e5m2": (ml_dtypes.float8_e5m2, 14)}[fmt]
    v = np.moveaxis(np.asarray(x, np.float32).astype(ml_dtypes.bfloat16).astype(np.float64), axis, -1)
    blocks = v.reshape(v.shape[:-1] + (-1, 32))
    amax = np.abs(blocks).max(-1, keepdims=True)
    byte = np.maximum(np.where(amax > 0, np.frexp(amax)[1] - 1 + 127, 0) - down, 1)
    scale = np.exp2(byte - 127.0)
    codes = (blocks / scale).astype(np.float32).astype(dtype).astype(np.float64)
    return np.moveaxis((codes * scale).reshape(v.shape), -1, axis)


WIDE = False


def mx_kscale(k):
    if not WIDE:
        return np.ones(k)
    levels = np.array([10, -10, 5, -5, 0])
    if k % 512:
        return np.exp2(np.random.permutation(np.resize(levels, k // 32))).repeat(32)
    a = np.empty((k // 512, 16))
    for p in range(k // 512):
        a[p, :8] = np.random.permutation(np.resize(levels, 8))
        for g in range(8):
            far = levels[np.abs(levels - a[p, g]) >= 10]
            a[p, g + 8] = far[np.random.randint(len(far))]
    return np.exp2(a.ravel()).repeat(32)


def f64(x):
    return np.asarray(x).astype(np.float64)


def striped(idx):
    return np.tile(idx.reshape(-1, 16).T, (8, 1)).astype(np.uint16)


def unstriped(offs):
    return offs[:16].T.reshape(-1).astype(np.int64)


E2M1 = np.array([0.0, 0.5, 1.0, 1.5, 2.0, 3.0, 4.0, 6.0, -0.0, -0.5, -1.0, -1.5, -2.0, -3.0, -4.0, -6.0])


def pack_weight(w, fmt):
    k, n = w.shape
    w = f64(np.asarray(w, np.float32).astype(ml_dtypes.bfloat16)).reshape(k // 32, 32, n)
    amax = np.abs(w).max(1)
    if fmt == "e4m3":
        byte = np.frexp(amax)[1] - 1 + 127 - 7
    else:
        mant, ex = np.frexp(amax / 6.0)
        byte = np.where(mant > 0.5, ex, ex - 1) + 127
    byte = np.clip(np.where(amax > 0, byte, 1), 1, 254)
    scaled = (w * np.exp2(127.0 - byte)[:, None, :]).reshape(k, n).astype(np.float32)
    by_word = np.ascontiguousarray(scaled.reshape(k // 512, 128, 4, n).transpose(0, 1, 3, 2))
    if fmt == "e4m3":
        words = by_word.astype(ml_dtypes.float8_e4m3fn).view(np.uint8)
    else:
        c = by_word.astype(ml_dtypes.float4_e2m1fn).view(np.uint8) & 0xF
        words = (c[..., 0::2] | (c[..., 1::2] << 4)).reshape(k // 512, 128, 2 * n)
    return np.ascontiguousarray(words), np.ascontiguousarray(byte.astype(np.uint8).reshape(k // 512, 16, n))


def unpack_weight(words, scales, fmt):
    g, _, n = scales.shape
    words = np.ascontiguousarray(words).reshape(g, 128, n, -1)
    if fmt == "e4m3":
        vals = words.view(ml_dtypes.float8_e4m3fn).astype(np.float64)
    else:
        nib = np.empty((g, 128, n, 4), np.uint8)
        nib[..., 0::2] = words & 0xF
        nib[..., 1::2] = words >> 4
        vals = E2M1[nib]
    vals = vals * np.repeat(np.exp2(scales.astype(np.float64) - 127.0), 8, axis=1)[..., None]
    return vals.transpose(0, 1, 3, 2).reshape(g * 512, n)


def relu(v):
    return np.maximum(v, 0.0)


K, T, E, C, H, N = 1536, 512, 4, 128, 512, 256
R = 4


def by_expert(wq, xq):
    return np.concatenate([wq[e].T @ xq[:, e * C:(e + 1) * C] for e in range(E)], axis=1)


def setup_inputs():
    n = np.random.standard_normal
    s = mx_kscale(K)[:, None]
    u = mx_kscale(H)
    slot_token = np.concatenate([r * (T // R) + np.random.permutation(T // R)[:C // R] for e in range(E) for r in range(R)])
    w1 = [pack_weight(m, "e2m1") for m in n((E, K, H)) / np.sqrt(K) / s[None]]
    w3 = [pack_weight(m, "e2m1") for m in n((E, K, H)) / np.sqrt(K) / s[None] * u[None, None, :]]
    w2 = [pack_weight(m, "e2m1") for m in n((E, H, N)) / np.sqrt(H) / u[None, :, None]]
    return {
        "xT": (n((K, T)) * s).astype(np.float32),
        "w1_words": np.stack([m[0] for m in w1]),
        "w1_scales": np.stack([m[1] for m in w1]),
        "w3_words": np.stack([m[0] for m in w3]),
        "w3_scales": np.stack([m[1] for m in w3]),
        "w2_words": np.stack([m[0] for m in w2]),
        "w2_scales": np.stack([m[1] for m in w2]),
        "offs": striped(slot_token),
    }


def reference(xT, w1_words, w1_scales, w3_words, w3_scales, w2_words, w2_scales, offs):
    idx = unstriped(offs)
    w1 = np.stack([unpack_weight(w1_words[e], w1_scales[e], "e2m1") for e in range(E)])
    w3 = np.stack([unpack_weight(w3_words[e], w3_scales[e], "e2m1") for e in range(E)])
    w2 = np.stack([unpack_weight(w2_words[e], w2_scales[e], "e2m1") for e in range(E)])
    xq = mxq(f64(xT)[:, idx], 0, "e4m3")
    h = relu(by_expert(w1, xq))
    h = h * by_expert(w3, xq)
    y = by_expert(w2, mxq(h, 0, "e4m3"))
    return y.reshape(N, E, R, C // R).transpose(0, 2, 1, 3).reshape(N, E * C)

@@ -1,0 +1,183 @@
+from contextlib import ExitStack
+
+import concourse.mybir as mybir
+from concourse.masks import make_identity
+
+K, T, E, C, H, N = 1536, 512, 4, 128, 512, 256
+R = 4
+P = 128
+PASSES = K // 512
+FLOPS = E * (2 * 2 * K * C * H + 2 * H * C * N)
+
+F32 = mybir.dt.float32
+BF16 = mybir.dt.bfloat16
+U32 = mybir.dt.uint32
+I32 = mybir.dt.int32
+U16 = mybir.dt.uint16
+U8 = mybir.dt.uint8
+E4M3 = mybir.dt.float8_e4m3fn_x4
+E2M1 = mybir.dt.float4_e2m1fn_x4
+COPY = mybir.ActivationFunctionType.Copy
+RELU = mybir.ActivationFunctionType.Relu
+MULT = mybir.AluOpType.mult
+
+CHUNKS = ((0, 0, 160, 256), (0, 256, 416, 512), (1, 0, 64, 512), (2, 0, 128, 512))
+
+
+def tile_moe_eps_glu_relu_kernel(
+    tc, xT, w1_words, w1_scales, w3_words, w3_scales, w2_words, w2_scales, offs, out
+):
+    nc = tc.nc
+    with ExitStack() as ctx:
+        keep = ctx.enter_context(tc.tile_pool(name="keep", bufs=1))
+        work = ctx.enter_context(tc.tile_pool(name="work", bufs=3))
+        psum = ctx.enter_context(tc.psum_pool(name="psum", bufs=3))
+        psum1 = ctx.enter_context(tc.psum_pool(name="psum1", bufs=1))
+
+        offsets = keep.tile([P, E * C // 16], U16, name="offsets")
+        x_raw = [keep.tile([P, 4, T], F32, name=f"x_raw{s}") for s in range(PASSES)]
+        x_grp = [keep.tile([P, T, 4], BF16, name=f"x_grp{s}", align_bytes=64) for s in range(PASSES)]
+        x_words = [keep.tile([P, T], U32, name=f"x_words{s}", align_bytes=64) for s in range(PASSES)]
+        x_bytes = [keep.tile([P, T], U8, name=f"x_bytes{s}", align_bytes=64) for s in range(PASSES)]
+        g_words = [keep.tile([P, E * C], U32, name=f"g_words{s}", align_bytes=64) for s in range(PASSES)]
+        g_bytes = [keep.tile([P, E * C], U8, name=f"g_bytes{s}", align_bytes=64) for s in range(PASSES)]
+        w13 = keep.tile([P, E, 2, PASSES, 2 * H], U8, name="w13", align_bytes=64)
+        w2_t = keep.tile([P, E, 2 * N], U8, name="w2_t", align_bytes=64)
+        sc13 = [keep.tile([P, 2, 2 * PASSES, H], U8, name=f"sc13_{f}", align_bytes=64) for f in range(2)]
+        sc2 = keep.tile([P, E, N], U8, name="sc2", align_bytes=64)
+        ident = keep.tile([P, P], F32, name="ident")
+        o_sb = keep.tile([P, 2, R, E, C // R], F32, name="o_sb")
+
+        nc.vector.memset(sc13[0][:].bitcast(I32), 0)
+        for s in range(PASSES):
+            nc.gpsimd.memset(x_bytes[s][:], 0)
+        nc.vector.memset(sc13[1][:].bitcast(I32), 0)
+        nc.vector.memset(sc2[:].bitcast(I32), 0)
+        nc.vector.memset(x_raw[2][:, :, 0:2], 0.0)
+        nc.vector.memset(w13[:].rearrange("p e m s c -> p (e m s) c").bitcast(I32)[:, :, 0:1], 0)
+        nc.vector.memset(w2_t[:].bitcast(I32)[:, :, 0:1], 0)
+        make_identity(nc, ident[:])
+
+        def load_x(s, a=0, b=T):
+            nc.sync.dma_start(
+                x_raw[s][:, :, a:b], xT[512 * s : 512 * (s + 1), a:b].rearrange("(p j) w -> p j w", j=4)
+            )
+
+        def load_w(m, e, s0=0, s1=PASSES):
+            words = (w1_words, w3_words)[m]
+            nc.sync.dma_start(
+                w13[:, e, m, s0:s1].bitcast(I32), words[e, s0:s1].bitcast(I32).rearrange("s p c -> p s c")
+            )
+
+        def load_sc13(f):
+            for m, scales in enumerate((w1_scales, w3_scales)):
+                src = scales[2 * f : 2 * f + 2].bitcast(I32).rearrange("e s (q r) c -> r q (e s) c", r=4)
+                dst = sc13[f][:].bitcast(I32)
+                for r in range(4):
+                    nc.sync.dma_start(dst[r:P:32, m, :, :], src[r])
+
+        def load_sc2():
+            src = w2_scales[:, 0].bitcast(I32).rearrange("e (q r) c -> r q e c", r=4)
+            dst = sc2[:].bitcast(I32)
+            for r in range(4):
+                nc.sync.dma_start(dst[r:P:32, :, :], src[r])
+
+        def load_w2():
+            nc.sync.dma_start(w2_t[:].bitcast(I32), w2_words[:, 0].bitcast(I32).rearrange("e p c -> p e c"))
+
+        nc.sync.dma_start(offsets[:], offs)
+        load_x(0, 0, 256)
+        load_x(0, 256, 512)
+        load_x(1)
+        load_sc13(0)
+        load_x(2)
+        load_w(0, 0, 0, 3)
+        load_w(1, 0, 0, 3)
+        load_w(0, 1, 0, 3)
+        load_w(1, 1, 0, 3)
+        load_sc13(1)
+        load_sc2()
+        load_w(0, 2, 0, 3)
+        load_w(1, 2, 0, 3)
+        load_w(0, 3, 0, 3)
+        load_w(1, 3, 0, 3)
+        load_w2()
+
+        def interleave(s, a, v, b):
+            dst = x_grp[s][:].rearrange("p (c i) t -> p c t i", i=4)
+            src = x_raw[s][:].rearrange("p t (c i) -> p c t i", i=4)
+            if v > a:
+                nc.vector.tensor_copy(dst[:, a // 4 : v // 4], src[:, a // 4 : v // 4])
+            if b > v:
+                nc.scalar.activation(dst[:, v // 4 : b // 4], src[:, v // 4 : b // 4], COPY)
+
+        def quantize(s, a, b):
+            nc.vector.quantize_mx(
+                out=x_words[s][:, a:b].bitcast(E4M3),
+                scales=x_bytes[s][:, a:b],
+                in_=x_grp[s][:, a:b].rearrange("p c t -> p (c t)"),
+            )
+
+        def gather(s, a, b):
+            lst = offsets[:, a // 16 : b // 16]
+            nc.vector.tensor_copy(g_words[s][:, a:b], x_words[s][:].indirect(lst))
+            nc.vector.tensor_copy(g_bytes[s][:, a:b], x_bytes[s][:].indirect(lst))
+
+        def product(e, m, name):
+            acc = psum.tile([P, H], F32, name=name)
+            cols = slice(C * e, C * (e + 1))
+            for s in range(PASSES):
+                nc.tensor.matmul_mx(
+                    out=acc[:],
+                    lhsT=g_words[s][:, cols].bitcast(E4M3),
+                    lhsT_scale=g_bytes[s][:, cols],
+                    rhs=w13[:, e, m, s, :].bitcast(E2M1),
+                    rhs_scale=sc13[e // 2][:, m, PASSES * (e % 2) + s, :],
+                    start=(s == 0),
+                    stop=(s == PASSES - 1),
+                )
+            return acc
+
+        def first_layer(e):
+            acc_a = product(e, 0, "acc_a")
+            act = work.tile([P, H], F32, name="act")
+            nc.scalar.activation(act[:], acc_a[:], RELU)
+            acc_b = product(e, 1, "acc_b")
+            h = work.tile([P, H], BF16, name="h")
+            nc.vector.tensor_tensor(h[:], acc_b[:], act[:], MULT)
+            return h
+
+        def second_layer(e, h):
+            turned = psum1.tile([P, 2, C], F32, name="turned")
+            words = h[:].bitcast(F32)
+            for u in range(2):
+                nc.tensor.transpose(turned[:, u, :], words[:, u::2], ident[:])
+            h_grp = work.tile([P, C, 4], BF16, name="h_grp", align_bytes=64)
+            h_flat = h_grp[:].rearrange("p c t -> p (c t)")
+            nc.scalar.copy(h_flat.bitcast(F32).rearrange("p (c u) -> p c u", u=2), turned[:].rearrange("p u c -> p c u"))
+            h_words = work.tile([P, C], U32, name="h_words", align_bytes=64)
+            h_bytes = work.tile([P, C], U8, name="h_bytes", align_bytes=64)
+            nc.vector.quantize_mx(out=h_words[:].bitcast(E4M3), scales=h_bytes[:], in_=h_flat)
+            y = psum1.tile([P, 2, C], F32, name="y")
+            for half in range(2):
+                nc.tensor.matmul_mx(
+                    out=y[:, half, :],
+                    lhsT=w2_t[:, e, 2 * P * half : 2 * P * (half + 1)].bitcast(E2M1),
+                    lhsT_scale=sc2[:, e, P * half : P * (half + 1)],
+                    rhs=h_words[:].bitcast(E4M3),
+                    rhs_scale=h_bytes[:],
+                    start=True,
+                    stop=True,
+                )
+            nc.scalar.copy(o_sb[:, :, :, e, :], y[:].rearrange("p h (m u) -> p h m u", m=R))
+
+        for s, a, v, b in CHUNKS:
+            interleave(s, a, v, b)
+            quantize(s, a, b)
+            if b == T:
+                gather(s, 0, 256)
+                gather(s, 256, 512)
+        for e in range(E):
+            second_layer(e, first_layer(e))
+        for half, queue in enumerate((nc.sync, nc.scalar)):
+            queue.dma_start(out[P * half : P * (half + 1), :], o_sb[:, half].rearrange("p m e u -> p (m e u)"))

@@ -21,7 +21,8 @@ COPY = mybir.ActivationFunctionType.Copy
 RELU = mybir.ActivationFunctionType.Relu
 MULT = mybir.AluOpType.mult
 
-CHUNKS = ((0, 0, 160, 256), (0, 256, 416, 512), (1, 0, 64, 512), (2, 0, 128, 512))
+KIB = 1024
+CHUNKS = ((0, 0, 160, 256), (0, 256, 416, 512), (1, 0, 128, 512), (2, 0, 96, 512))
 
 
 def tile_moe_eps_glu_relu_kernel(
@@ -30,154 +31,161 @@ def tile_moe_eps_glu_relu_kernel(
     nc = tc.nc
     with ExitStack() as ctx:
         keep = ctx.enter_context(tc.tile_pool(name="keep", bufs=1))
-        work = ctx.enter_context(tc.tile_pool(name="work", bufs=3))
-        psum = ctx.enter_context(tc.psum_pool(name="psum", bufs=3))
+        turns = ctx.enter_context(tc.tile_pool(name="turns", bufs=1))
+        work = ctx.enter_context(tc.tile_pool(name="work", bufs=2))
+        psum = ctx.enter_context(tc.psum_pool(name="psum", bufs=2))
         psum1 = ctx.enter_context(tc.psum_pool(name="psum1", bufs=1))
 
+        def shared(shape, dtype, name, kib):
+            return turns.tile(shape, dtype, name=name, align_bytes=64, offset=int(kib * KIB))
+
         offsets = keep.tile([P, E * C // 16], U16, name="offsets")
-        x_raw = [keep.tile([P, 4, T], F32, name=f"x_raw{s}") for s in range(PASSES)]
-        x_grp = [keep.tile([P, T, 4], BF16, name=f"x_grp{s}", align_bytes=64) for s in range(PASSES)]
         x_words = [keep.tile([P, T], U32, name=f"x_words{s}", align_bytes=64) for s in range(PASSES)]
         x_bytes = [keep.tile([P, T], U8, name=f"x_bytes{s}", align_bytes=64) for s in range(PASSES)]
-        g_words = [keep.tile([P, E * C], U32, name=f"g_words{s}", align_bytes=64) for s in range(PASSES)]
-        g_bytes = [keep.tile([P, E * C], U8, name=f"g_bytes{s}", align_bytes=64) for s in range(PASSES)]
-        w13 = keep.tile([P, E, 2, PASSES, 2 * H], U8, name="w13", align_bytes=64)
-        w2_t = keep.tile([P, E, 2 * N], U8, name="w2_t", align_bytes=64)
-        sc13 = [keep.tile([P, 2, 2 * PASSES, H], U8, name=f"sc13_{f}", align_bytes=64) for f in range(2)]
+        sc13 = [keep.tile([P, E * PASSES, H], U8, name=f"sc13_{m}", align_bytes=64) for m in range(2)]
         sc2 = keep.tile([P, E, N], U8, name="sc2", align_bytes=64)
+        h_words = [keep.tile([P, C], U32, name=f"h_words{e}", align_bytes=64) for e in range(E)]
+        h_bytes = [keep.tile([P, C], U8, name=f"h_bytes{e}", align_bytes=64) for e in range(E)]
+        act = [keep.tile([P, H], F32, name=f"act{e}") for e in range(E)]
         ident = keep.tile([P, P], F32, name="ident")
-        o_sb = keep.tile([P, 2, R, E, C // R], F32, name="o_sb")
+        o_sb = [keep.tile([P, R, E, C // R], F32, name=f"o_sb{half}") for half in range(2)]
 
-        nc.vector.memset(sc13[0][:].bitcast(I32), 0)
-        for s in range(PASSES):
-            nc.gpsimd.memset(x_bytes[s][:], 0)
-        nc.vector.memset(sc13[1][:].bitcast(I32), 0)
-        nc.vector.memset(sc2[:].bitcast(I32), 0)
-        nc.vector.memset(x_raw[2][:, :, 0:2], 0.0)
-        nc.vector.memset(w13[:].rearrange("p e m s c -> p (e m s) c").bitcast(I32)[:, :, 0:1], 0)
-        nc.vector.memset(w2_t[:].bitcast(I32)[:, :, 0:1], 0)
+        for plane in (sc13[0], x_bytes[0], sc13[1], sc2, x_bytes[1], x_bytes[2]):
+            nc.vector.memset(plane[:].bitcast(I32), 0)
         make_identity(nc, ident[:])
 
-        def load_x(s, a=0, b=T):
-            nc.sync.dma_start(
-                x_raw[s][:, :, a:b], xT[512 * s : 512 * (s + 1), a:b].rearrange("(p j) w -> p j w", j=4)
-            )
+        raw_at = (0, 4, 8, 16)
+        grp_at = (24, 28, 32)
 
-        def load_w(m, e, s0=0, s1=PASSES):
+        nc.sync.dma_start(offsets[:], offs)
+        x_raw = []
+        for i, (s, a, v, b) in enumerate(CHUNKS):
+            raw = shared([P, 4, b - a], F32, f"x_raw{i}", raw_at[i])
+            nc.sync.dma_start(raw[:], xT[512 * s : 512 * (s + 1), a:b].rearrange("(p j) w -> p j w", j=4))
+            x_raw.append(raw)
+
+        w13 = {}
+
+        def load_w13(home, e, m, cuts=(0, PASSES)):
             words = (w1_words, w3_words)[m]
-            nc.sync.dma_start(
-                w13[:, e, m, s0:s1].bitcast(I32), words[e, s0:s1].bitcast(I32).rearrange("s p c -> p s c")
-            )
+            for a, b in zip(cuts, cuts[1:]):
+                nc.sync.dma_start(home[:, a:b].bitcast(I32), words[e, a:b].bitcast(I32).rearrange("s p c -> p s c"))
+            w13[e, m] = home
 
-        def load_sc13(f):
-            for m, scales in enumerate((w1_scales, w3_scales)):
-                src = scales[2 * f : 2 * f + 2].bitcast(I32).rearrange("e s (q r) c -> r q (e s) c", r=4)
-                dst = sc13[f][:].bitcast(I32)
-                for r in range(4):
-                    nc.sync.dma_start(dst[r:P:32, m, :, :], src[r])
+        for e in range(2):
+            load_w13(keep.tile([P, PASSES, 2 * H], U8, name=f"w1_{e}", align_bytes=64), e, 0)
 
-        def load_sc2():
-            src = w2_scales[:, 0].bitcast(I32).rearrange("e (q r) c -> r q e c", r=4)
-            dst = sc2[:].bitcast(I32)
+        for plane, scales in ((sc13[0], w1_scales), (sc13[1], w3_scales), (sc2, w2_scales)):
+            src = scales.bitcast(I32).rearrange("e s (q r) c -> r q (e s) c", r=4)
+            dst = plane[:].bitcast(I32)
             for r in range(4):
                 nc.sync.dma_start(dst[r:P:32, :, :], src[r])
 
-        def load_w2():
-            nc.sync.dma_start(w2_t[:].bitcast(I32), w2_words[:, 0].bitcast(I32).rearrange("e p c -> p e c"))
+        g_words, g_bytes = {}, {}
 
-        nc.sync.dma_start(offsets[:], offs)
-        load_x(0, 0, 256)
-        load_x(0, 256, 512)
-        load_x(1)
-        load_sc13(0)
-        load_x(2)
-        load_w(0, 0, 0, 3)
-        load_w(1, 0, 0, 3)
-        load_w(0, 1, 0, 3)
-        load_w(1, 1, 0, 3)
-        load_sc13(1)
-        load_sc2()
-        load_w(0, 2, 0, 3)
-        load_w(1, 2, 0, 3)
-        load_w(0, 3, 0, 3)
-        load_w(1, 3, 0, 3)
-        load_w2()
+        def gather(s, pair, words, planes):
+            lst = offsets[:, 16 * pair : 16 * (pair + 1)]
+            nc.vector.tensor_copy(words[:], x_words[s][:].indirect(lst))
+            nc.vector.tensor_copy(planes[:], x_bytes[s][:].indirect(lst))
+            g_words[s, pair], g_bytes[s, pair] = words, planes
 
-        def interleave(s, a, v, b):
-            dst = x_grp[s][:].rearrange("p (c i) t -> p c t i", i=4)
-            src = x_raw[s][:].rearrange("p t (c i) -> p c t i", i=4)
-            if v > a:
-                nc.vector.tensor_copy(dst[:, a // 4 : v // 4], src[:, a // 4 : v // 4])
-            if b > v:
-                nc.scalar.activation(dst[:, v // 4 : b // 4], src[:, v // 4 : b // 4], COPY)
+        def gather_kept(s, pair):
+            gather(
+                s,
+                pair,
+                keep.tile([P, 2 * C], U32, name=f"g_words{s}{pair}", align_bytes=64),
+                keep.tile([P, 2 * C], U8, name=f"g_bytes{s}{pair}", align_bytes=64),
+            )
 
-        def quantize(s, a, b):
+        x_grp = [shared([P, T, 4], BF16, f"x_grp{s}", grp_at[s]) for s in range(PASSES)]
+        for i, (s, a, v, b) in enumerate(CHUNKS):
+            dst = x_grp[s][:, a:b].rearrange("p (c i) t -> p c t i", i=4)
+            src = x_raw[i][:].rearrange("p t (c i) -> p c t i", i=4)
+            cut = (v - a) // 4
+            nc.vector.tensor_copy(dst[:, :cut], src[:, :cut])
+            nc.scalar.activation(dst[:, cut:], src[:, cut:], COPY)
             nc.vector.quantize_mx(
                 out=x_words[s][:, a:b].bitcast(E4M3),
                 scales=x_bytes[s][:, a:b],
                 in_=x_grp[s][:, a:b].rearrange("p c t -> p (c t)"),
             )
+            if b == T:
+                gather_kept(s, 0)
+                if s == 0:
+                    gather_kept(s, 1)
+        for s in (1, 2):
+            gather(
+                s,
+                1,
+                shared([P, 2 * C], U32, f"g_words{s}1", grp_at[2] + 2 * (s - 1)),
+                shared([P, 2 * C], U8, f"g_bytes{s}1", grp_at[2] + 2 * (s - 1) + 1),
+            )
 
-        def gather(s, a, b):
-            lst = offsets[:, a // 16 : b // 16]
-            nc.vector.tensor_copy(g_words[s][:, a:b], x_words[s][:].indirect(lst))
-            nc.vector.tensor_copy(g_bytes[s][:, a:b], x_bytes[s][:].indirect(lst))
+        for (e, m), at in (((0, 1), raw_at[0]), ((1, 1), raw_at[1]), ((2, 0), grp_at[0]), ((3, 0), raw_at[2]), ((2, 1), raw_at[2] + 4)):
+            load_w13(shared([P, PASSES, 2 * H], U8, f"w13_{e}{m}", at), e, m)
+        load_w13(shared([P, PASSES, 2 * H], U8, "w13_31", grp_at[1]), 3, 1, cuts=(0, PASSES - 1, PASSES))
+        w2_t = shared([P, E, 2 * N], U8, "w2_t", raw_at[3])
+        nc.sync.dma_start(w2_t[:].bitcast(I32), w2_words[:, 0].bitcast(I32).rearrange("e p c -> p e c"))
 
         def product(e, m, name):
             acc = psum.tile([P, H], F32, name=name)
-            cols = slice(C * e, C * (e + 1))
+            cols = slice(C * (e % 2), C * (e % 2 + 1))
             for s in range(PASSES):
                 nc.tensor.matmul_mx(
                     out=acc[:],
-                    lhsT=g_words[s][:, cols].bitcast(E4M3),
-                    lhsT_scale=g_bytes[s][:, cols],
-                    rhs=w13[:, e, m, s, :].bitcast(E2M1),
-                    rhs_scale=sc13[e // 2][:, m, PASSES * (e % 2) + s, :],
+                    lhsT=g_words[s, e // 2][:, cols].bitcast(E4M3),
+                    lhsT_scale=g_bytes[s, e // 2][:, cols],
+                    rhs=w13[e, m][:, s, :].bitcast(E2M1),
+                    rhs_scale=sc13[m][:, PASSES * e + s, :],
                     start=(s == 0),
                     stop=(s == PASSES - 1),
                 )
             return acc
 
-        def first_layer(e):
-            acc_a = product(e, 0, "acc_a")
-            act = work.tile([P, H], F32, name="act")
-            nc.scalar.activation(act[:], acc_a[:], RELU)
-            acc_b = product(e, 1, "acc_b")
+        def gate(e):
+            nc.scalar.activation(act[e][:], product(e, 0, "acc_a")[:], RELU)
+
+        def hidden(e):
             h = work.tile([P, H], BF16, name="h")
-            nc.vector.tensor_tensor(h[:], acc_b[:], act[:], MULT)
+            nc.vector.tensor_tensor(h[:], product(e, 1, "acc_b")[:], act[e][:], MULT)
             return h
 
-        def second_layer(e, h):
-            turned = psum1.tile([P, 2, C], F32, name="turned")
+        def turn(e, h):
+            turned = psum.tile([P, 2, C], F32, name="turned")
             words = h[:].bitcast(F32)
             for u in range(2):
                 nc.tensor.transpose(turned[:, u, :], words[:, u::2], ident[:])
             h_grp = work.tile([P, C, 4], BF16, name="h_grp", align_bytes=64)
             h_flat = h_grp[:].rearrange("p c t -> p (c t)")
             nc.scalar.copy(h_flat.bitcast(F32).rearrange("p (c u) -> p c u", u=2), turned[:].rearrange("p u c -> p c u"))
-            h_words = work.tile([P, C], U32, name="h_words", align_bytes=64)
-            h_bytes = work.tile([P, C], U8, name="h_bytes", align_bytes=64)
-            nc.vector.quantize_mx(out=h_words[:].bitcast(E4M3), scales=h_bytes[:], in_=h_flat)
-            y = psum1.tile([P, 2, C], F32, name="y")
-            for half in range(2):
-                nc.tensor.matmul_mx(
-                    out=y[:, half, :],
-                    lhsT=w2_t[:, e, 2 * P * half : 2 * P * (half + 1)].bitcast(E2M1),
-                    lhsT_scale=sc2[:, e, P * half : P * (half + 1)],
-                    rhs=h_words[:].bitcast(E4M3),
-                    rhs_scale=h_bytes[:],
-                    start=True,
-                    stop=True,
-                )
-            nc.scalar.copy(o_sb[:, :, :, e, :], y[:].rearrange("p h (m u) -> p h m u", m=R))
+            nc.vector.quantize_mx(out=h_words[e][:].bitcast(E4M3), scales=h_bytes[e][:], in_=h_flat)
 
-        for s, a, v, b in CHUNKS:
-            interleave(s, a, v, b)
-            quantize(s, a, b)
-            if b == T:
-                gather(s, 0, 256)
-                gather(s, 256, 512)
-        for e in range(E):
-            second_layer(e, first_layer(e))
-        for half, queue in enumerate((nc.sync, nc.scalar)):
-            queue.dma_start(out[P * half : P * (half + 1), :], o_sb[:, half].rearrange("p m e u -> p (m e u)"))
+        for pair in range(2):
+            first, second = 2 * pair, 2 * pair + 1
+            gate(first)
+            gate(second)
+            hs = [hidden(first), hidden(second)]
+            turn(first, hs[0])
+            turn(second, hs[1])
+
+        copies = (nc.vector.tensor_copy, nc.scalar.copy)
+        for pair in range(2):
+            for half, queue in enumerate((nc.sync, nc.scalar)):
+                if pair == 0:
+                    y = psum1.tile([P, 2, C], F32, name=f"y_early{half}")
+                else:
+                    y = psum.tile([P, 2, C], F32, name=f"y_last{half}", tag="acc_a")
+                for i in range(2):
+                    e = 2 * pair + i
+                    nc.tensor.matmul_mx(
+                        out=y[:, i, :],
+                        lhsT=w2_t[:, e, 2 * P * half : 2 * P * (half + 1)].bitcast(E2M1),
+                        lhsT_scale=sc2[:, e, P * half : P * (half + 1)],
+                        rhs=h_words[e][:].bitcast(E4M3),
+                        rhs_scale=h_bytes[e][:],
+                        start=True,
+                        stop=True,
+                    )
+                copies[half](o_sb[half][:, :, 2 * pair : 2 * pair + 2, :], y[:].rearrange("p e (m u) -> p m e u", m=R))
+                if pair == 1:
+                    queue.dma_start(out[P * half : P * (half + 1), :], o_sb[half][:].rearrange("p m e u -> p (m e u)"))

@@ -22,7 +22,7 @@ RELU = mybir.ActivationFunctionType.Relu
 MULT = mybir.AluOpType.mult
 
 KIB = 1024
-CHUNKS = ((0, 0, 160, 256), (0, 256, 416, 512), (1, 0, 128, 512), (2, 0, 96, 512))
+CHUNKS = ((0, 0, 320, 512), (1, 0, 64, 512), (2, 0, 96, 512))
 
 
 def tile_moe_eps_glu_relu_kernel(
@@ -43,18 +43,19 @@ def tile_moe_eps_glu_relu_kernel(
         x_words = [keep.tile([P, T], U32, name=f"x_words{s}", align_bytes=64) for s in range(PASSES)]
         x_bytes = [keep.tile([P, T], U8, name=f"x_bytes{s}", align_bytes=64) for s in range(PASSES)]
         sc13 = [keep.tile([P, E * PASSES, H], U8, name=f"sc13_{m}", align_bytes=64) for m in range(2)]
-        sc2 = keep.tile([P, E, N], U8, name="sc2", align_bytes=64)
+        sc2 = sc13[0][:, 0:2, :].rearrange("p s (a c) -> p (s a) c", c=N)
         h_words = [keep.tile([P, C], U32, name=f"h_words{e}", align_bytes=64) for e in range(E)]
         h_bytes = [keep.tile([P, C], U8, name=f"h_bytes{e}", align_bytes=64) for e in range(E)]
-        act = [keep.tile([P, H], F32, name=f"act{e}") for e in range(E)]
+        act_at = 36
+        act = [shared([P, 2, P, 2], F32, f"act{e}", act_at + 2 * e) for e in range(E)]
         ident = keep.tile([P, P], F32, name="ident")
         o_sb = [keep.tile([P, R, E, C // R], F32, name=f"o_sb{half}") for half in range(2)]
 
-        for plane in (sc13[0], x_bytes[0], sc13[1], sc2, x_bytes[1], x_bytes[2]):
+        for plane in (sc13[0], x_bytes[0], sc13[1], x_bytes[1], x_bytes[2]):
             nc.vector.memset(plane[:].bitcast(I32), 0)
         make_identity(nc, ident[:])
 
-        raw_at = (0, 4, 8, 16)
+        raw_at = (0, 8, 16)
         grp_at = (24, 28, 32)
 
         nc.sync.dma_start(offsets[:], offs)
@@ -72,27 +73,39 @@ def tile_moe_eps_glu_relu_kernel(
                 nc.sync.dma_start(home[:, a:b].bitcast(I32), words[e, a:b].bitcast(I32).rearrange("s p c -> p s c"))
             w13[e, m] = home
 
-        for e in range(2):
-            load_w13(keep.tile([P, PASSES, 2 * H], U8, name=f"w1_{e}", align_bytes=64), e, 0)
+        load_w13(keep.tile([P, PASSES, 2 * H], U8, name="w13_00", align_bytes=64), 0, 0)
 
-        for plane, scales in ((sc13[0], w1_scales), (sc13[1], w3_scales), (sc2, w2_scales)):
+        def load_scales(plane, scales):
             src = scales.bitcast(I32).rearrange("e s (q r) c -> r q (e s) c", r=4)
-            dst = plane[:].bitcast(I32)
+            dst = plane.bitcast(I32)
             for r in range(4):
                 nc.sync.dma_start(dst[r:P:32, :, :], src[r])
 
+        load_scales(sc13[0][:], w1_scales)
+        load_scales(sc13[1][:], w3_scales)
+
         g_words, g_bytes = {}, {}
 
-        def gather(s, pair, words, planes):
-            lst = offsets[:, 16 * pair : 16 * (pair + 1)]
+        def gather(s, experts, words, planes):
+            lst = offsets[:, experts[0] * C // 16 : (experts[-1] + 1) * C // 16]
             nc.vector.tensor_copy(words[:], x_words[s][:].indirect(lst))
             nc.vector.tensor_copy(planes[:], x_bytes[s][:].indirect(lst))
-            g_words[s, pair], g_bytes[s, pair] = words, planes
+            for i, e in enumerate(experts):
+                g_words[s, e], g_bytes[s, e] = words[:, C * i : C * (i + 1)], planes[:, C * i : C * (i + 1)]
+
+        def gather_late(e, at):
+            for s in (1, 2):
+                gather(
+                    s,
+                    (e,),
+                    shared([P, C], U32, f"g_words{s}{e}", at + s - 1),
+                    shared([P, C], U8, f"g_bytes{s}{e}", at + s - 0.5),
+                )
 
         def gather_kept(s, pair):
             gather(
                 s,
-                pair,
+                (2 * pair, 2 * pair + 1),
                 keep.tile([P, 2 * C], U32, name=f"g_words{s}{pair}", align_bytes=64),
                 keep.tile([P, 2 * C], U8, name=f"g_bytes{s}{pair}", align_bytes=64),
             )
@@ -113,28 +126,22 @@ def tile_moe_eps_glu_relu_kernel(
                 gather_kept(s, 0)
                 if s == 0:
                     gather_kept(s, 1)
-        for s in (1, 2):
-            gather(
-                s,
-                1,
-                shared([P, 2 * C], U32, f"g_words{s}1", grp_at[2] + 2 * (s - 1)),
-                shared([P, 2 * C], U8, f"g_bytes{s}1", grp_at[2] + 2 * (s - 1) + 1),
-            )
+        gather_late(2, grp_at[2])
 
-        for (e, m), at in (((0, 1), raw_at[0]), ((1, 1), raw_at[1]), ((2, 0), grp_at[0]), ((3, 0), raw_at[2]), ((2, 1), raw_at[2] + 4)):
+        homes = (raw_at[0], raw_at[0] + 3, grp_at[0], raw_at[1], raw_at[1] + 3, raw_at[2])
+        for (e, m), at in zip(((0, 1), (1, 0), (1, 1), (2, 0), (3, 0), (2, 1)), homes):
             load_w13(shared([P, PASSES, 2 * H], U8, f"w13_{e}{m}", at), e, m)
-        load_w13(shared([P, PASSES, 2 * H], U8, "w13_31", grp_at[1]), 3, 1, cuts=(0, PASSES - 1, PASSES))
-        w2_t = shared([P, E, 2 * N], U8, "w2_t", raw_at[3])
+        load_w13(shared([P, PASSES, 2 * H], U8, "w13_31", raw_at[2] + 3), 3, 1, cuts=(0, PASSES - 1, PASSES))
+        w2_t = shared([P, E, 2 * N], U8, "w2_t", raw_at[2] + 6)
         nc.sync.dma_start(w2_t[:].bitcast(I32), w2_words[:, 0].bitcast(I32).rearrange("e p c -> p e c"))
 
         def product(e, m, name):
             acc = psum.tile([P, H], F32, name=name)
-            cols = slice(C * (e % 2), C * (e % 2 + 1))
             for s in range(PASSES):
                 nc.tensor.matmul_mx(
                     out=acc[:],
-                    lhsT=g_words[s, e // 2][:, cols].bitcast(E4M3),
-                    lhsT_scale=g_bytes[s, e // 2][:, cols],
+                    lhsT=g_words[s, e].bitcast(E4M3),
+                    lhsT_scale=g_bytes[s, e],
                     rhs=w13[e, m][:, s, :].bitcast(E2M1),
                     rhs_scale=sc13[m][:, PASSES * e + s, :],
                     start=(s == 0),
@@ -142,31 +149,41 @@ def tile_moe_eps_glu_relu_kernel(
                 )
             return acc
 
+        def by_half(acc):
+            return acc[:].rearrange("p (q u d) -> p u q d", u=2, d=2)
+
         def gate(e):
-            nc.scalar.activation(act[e][:], product(e, 0, "acc_a")[:], RELU)
+            nc.scalar.activation(act[e][:], by_half(product(e, 0, "acc_a")), RELU)
 
         def hidden(e):
-            h = work.tile([P, H], BF16, name="h")
-            nc.vector.tensor_tensor(h[:], product(e, 1, "acc_b")[:], act[e][:], MULT)
+            h = work.tile([P, 2, P, 2], BF16, name="h")
+            nc.vector.tensor_tensor(h[:], by_half(product(e, 1, "acc_b")), act[e][:], MULT)
             return h
 
         def turn(e, h):
             turned = psum.tile([P, 2, C], F32, name="turned")
             words = h[:].bitcast(F32)
             for u in range(2):
-                nc.tensor.transpose(turned[:, u, :], words[:, u::2], ident[:])
+                nc.tensor.transpose(turned[:, u, :], words[:, u, :, 0], ident[:])
             h_grp = work.tile([P, C, 4], BF16, name="h_grp", align_bytes=64)
             h_flat = h_grp[:].rearrange("p c t -> p (c t)")
             nc.scalar.copy(h_flat.bitcast(F32).rearrange("p (c u) -> p c u", u=2), turned[:].rearrange("p u c -> p c u"))
             nc.vector.quantize_mx(out=h_words[e][:].bitcast(E4M3), scales=h_bytes[e][:], in_=h_flat)
 
-        for pair in range(2):
-            first, second = 2 * pair, 2 * pair + 1
-            gate(first)
-            gate(second)
-            hs = [hidden(first), hidden(second)]
-            turn(first, hs[0])
-            turn(second, hs[1])
+        gate(0)
+        h0 = hidden(0)
+        gather_late(3, act_at)
+        gate(1)
+        turn(0, h0)
+        h1 = hidden(1)
+        gate(2)
+        turn(1, h1)
+        gate(3)
+        load_scales(sc2, w2_scales)
+        h2 = hidden(2)
+        h3 = hidden(3)
+        turn(2, h2)
+        turn(3, h3)
 
         copies = (nc.vector.tensor_copy, nc.scalar.copy)
         for pair in range(2):

@@ -22,7 +22,7 @@ RELU = mybir.ActivationFunctionType.Relu
 MULT = mybir.AluOpType.mult
 
 KIB = 1024
-CHUNKS = ((0, 0, 320, 512), (1, 0, 64, 512), (2, 0, 96, 512))
+CHUNKS = ((0, 0, 160, 256), (0, 256, 416, 512), (1, 0, 128, 512), (2, 0, 0, 512))
 
 
 def tile_moe_eps_glu_relu_kernel(
@@ -32,7 +32,7 @@ def tile_moe_eps_glu_relu_kernel(
     with ExitStack() as ctx:
         keep = ctx.enter_context(tc.tile_pool(name="keep", bufs=1))
         turns = ctx.enter_context(tc.tile_pool(name="turns", bufs=1))
-        work = ctx.enter_context(tc.tile_pool(name="work", bufs=2))
+        work = ctx.enter_context(tc.tile_pool(name="work", bufs=3))
         psum = ctx.enter_context(tc.psum_pool(name="psum", bufs=2))
         psum1 = ctx.enter_context(tc.psum_pool(name="psum1", bufs=1))
 
@@ -42,12 +42,10 @@ def tile_moe_eps_glu_relu_kernel(
         offsets = keep.tile([P, E * C // 16], U16, name="offsets")
         x_words = [keep.tile([P, T], U32, name=f"x_words{s}", align_bytes=64) for s in range(PASSES)]
         x_bytes = [keep.tile([P, T], U8, name=f"x_bytes{s}", align_bytes=64) for s in range(PASSES)]
-        sc13 = [keep.tile([P, E * PASSES, H], U8, name=f"sc13_{m}", align_bytes=64) for m in range(2)]
-        sc2 = sc13[0][:, 0:2, :].rearrange("p s (a c) -> p (s a) c", c=N)
-        h_words = [keep.tile([P, C], U32, name=f"h_words{e}", align_bytes=64) for e in range(E)]
-        h_bytes = [keep.tile([P, C], U8, name=f"h_bytes{e}", align_bytes=64) for e in range(E)]
-        act_at = 36
-        act = [shared([P, 2, P, 2], F32, f"act{e}", act_at + 2 * e) for e in range(E)]
+        sc13 = [keep.tile([P, E * PASSES * H], U8, name=f"sc13_{m}", align_bytes=64) for m in range(2)]
+        sc2 = sc13[0][:, : E * N]
+        h_words, h_bytes = {}, {}
+        act = [keep.tile([P, 2, P, 2], F32, name=f"act{e}") for e in range(E)]
         ident = keep.tile([P, P], F32, name="ident")
         o_sb = [keep.tile([P, R, E, C // R], F32, name=f"o_sb{half}") for half in range(2)]
 
@@ -55,7 +53,7 @@ def tile_moe_eps_glu_relu_kernel(
             nc.vector.memset(plane[:].bitcast(I32), 0)
         make_identity(nc, ident[:])
 
-        raw_at = (0, 8, 16)
+        raw_at = (0, 4, 8, 16)
         grp_at = (24, 28, 32)
 
         nc.sync.dma_start(offsets[:], offs)
@@ -67,22 +65,25 @@ def tile_moe_eps_glu_relu_kernel(
 
         w13 = {}
 
-        def load_w13(home, e, m, cuts=(0, PASSES)):
-            words = (w1_words, w3_words)[m]
-            for a, b in zip(cuts, cuts[1:]):
-                nc.sync.dma_start(home[:, a:b].bitcast(I32), words[e, a:b].bitcast(I32).rearrange("s p c -> p s c"))
-            w13[e, m] = home
+        def load_w13(m, experts, passes, at):
+            shape, name = [P, len(experts) * len(passes), 2 * H], f"w13_{m}{experts[0]}{passes[0]}"
+            home = keep.tile(shape, U8, name=name, align_bytes=64) if at is None else shared(shape, U8, name, at)
+            words = (w1_words, w3_words)[m][experts[0] : experts[-1] + 1, passes[0] : passes[-1] + 1]
+            nc.sync.dma_start(home[:].bitcast(I32), words.bitcast(I32).rearrange("e s p c -> p (e s) c"))
+            for i, (e, s) in enumerate((e, s) for e in experts for s in passes):
+                w13[e, m, s] = home[:, i, :]
 
-        load_w13(keep.tile([P, PASSES, 2 * H], U8, name="w13_00", align_bytes=64), 0, 0)
+        for e in range(2):
+            load_w13(0, (e,), (0, 1), None)
 
-        def load_scales(plane, scales):
+        def load_scales(plane, scales, rows):
             src = scales.bitcast(I32).rearrange("e s (q r) c -> r q (e s) c", r=4)
-            dst = plane.bitcast(I32)
+            dst = plane.bitcast(I32).rearrange("p (a c) -> p a c", a=rows)
             for r in range(4):
                 nc.sync.dma_start(dst[r:P:32, :, :], src[r])
 
-        load_scales(sc13[0][:], w1_scales)
-        load_scales(sc13[1][:], w3_scales)
+        load_scales(sc13[0][:], w1_scales, E * PASSES)
+        load_scales(sc13[1][:], w3_scales, E * PASSES)
 
         g_words, g_bytes = {}, {}
 
@@ -92,15 +93,6 @@ def tile_moe_eps_glu_relu_kernel(
             nc.vector.tensor_copy(planes[:], x_bytes[s][:].indirect(lst))
             for i, e in enumerate(experts):
                 g_words[s, e], g_bytes[s, e] = words[:, C * i : C * (i + 1)], planes[:, C * i : C * (i + 1)]
-
-        def gather_late(e, at):
-            for s in (1, 2):
-                gather(
-                    s,
-                    (e,),
-                    shared([P, C], U32, f"g_words{s}{e}", at + s - 1),
-                    shared([P, C], U8, f"g_bytes{s}{e}", at + s - 0.5),
-                )
 
         def gather_kept(s, pair):
             gather(
@@ -115,7 +107,8 @@ def tile_moe_eps_glu_relu_kernel(
             dst = x_grp[s][:, a:b].rearrange("p (c i) t -> p c t i", i=4)
             src = x_raw[i][:].rearrange("p t (c i) -> p c t i", i=4)
             cut = (v - a) // 4
-            nc.vector.tensor_copy(dst[:, :cut], src[:, :cut])
+            if cut:
+                nc.vector.tensor_copy(dst[:, :cut], src[:, :cut])
             nc.scalar.activation(dst[:, cut:], src[:, cut:], COPY)
             nc.vector.quantize_mx(
                 out=x_words[s][:, a:b].bitcast(E4M3),
@@ -124,15 +117,18 @@ def tile_moe_eps_glu_relu_kernel(
             )
             if b == T:
                 gather_kept(s, 0)
-                if s == 0:
-                    gather_kept(s, 1)
-        gather_late(2, grp_at[2])
+                gather_kept(s, 1)
 
-        homes = (raw_at[0], raw_at[0] + 3, grp_at[0], raw_at[1], raw_at[1] + 3, raw_at[2])
-        for (e, m), at in zip(((0, 1), (1, 0), (1, 1), (2, 0), (3, 0), (2, 1)), homes):
-            load_w13(shared([P, PASSES, 2 * H], U8, f"w13_{e}{m}", at), e, m)
-        load_w13(shared([P, PASSES, 2 * H], U8, "w13_31", raw_at[2] + 3), 3, 1, cuts=(0, PASSES - 1, PASSES))
-        w2_t = shared([P, E, 2 * N], U8, "w2_t", raw_at[2] + 6)
+        load_w13(1, (0,), (0, 1), raw_at[0])
+        load_w13(1, (1,), (0, 1), raw_at[0] + 2)
+        load_w13(0, (0, 1), (2,), raw_at[1])
+        load_w13(1, (0, 1), (2,), raw_at[1] + 2)
+        load_w13(0, (2,), (0, 1, 2), raw_at[2])
+        load_w13(0, (3,), (0, 1, 2), raw_at[2] + 3)
+        load_w13(1, (2,), (0, 1, 2), raw_at[3])
+        load_w13(1, (3,), (0, 1), raw_at[3] + 3)
+        load_w13(1, (3,), (2,), raw_at[3] + 5)
+        w2_t = shared([P, E, 2 * N], U8, "w2_t", raw_at[3] + 6)
         nc.sync.dma_start(w2_t[:].bitcast(I32), w2_words[:, 0].bitcast(I32).rearrange("e p c -> p e c"))
 
         def product(e, m, name):
@@ -142,8 +138,8 @@ def tile_moe_eps_glu_relu_kernel(
                     out=acc[:],
                     lhsT=g_words[s, e].bitcast(E4M3),
                     lhsT_scale=g_bytes[s, e],
-                    rhs=w13[e, m][:, s, :].bitcast(E2M1),
-                    rhs_scale=sc13[m][:, PASSES * e + s, :],
+                    rhs=w13[e, m, s].bitcast(E2M1),
+                    rhs_scale=sc13[m][:, H * (PASSES * e + s) : H * (PASSES * e + s + 1)],
                     start=(s == 0),
                     stop=(s == PASSES - 1),
                 )
@@ -157,52 +153,60 @@ def tile_moe_eps_glu_relu_kernel(
 
         def hidden(e):
             h = work.tile([P, 2, P, 2], BF16, name="h")
-            nc.vector.tensor_tensor(h[:], by_half(product(e, 1, "acc_b")), act[e][:], MULT)
+            acc = by_half(product(e, 1, "acc_b"))
+            for a, b in ((0, 1), (1, 2)) if e == E - 1 else ((0, 2),):
+                nc.vector.tensor_tensor(h[:, a:b], acc[:, a:b], act[e][:, a:b], MULT)
             return h
 
-        def turn(e, h):
-            turned = psum.tile([P, 2, C], F32, name="turned")
-            words = h[:].bitcast(F32)
-            for u in range(2):
-                nc.tensor.transpose(turned[:, u, :], words[:, u, :, 0], ident[:])
-            h_grp = work.tile([P, C, 4], BF16, name="h_grp", align_bytes=64)
-            h_flat = h_grp[:].rearrange("p c t -> p (c t)")
-            nc.scalar.copy(h_flat.bitcast(F32).rearrange("p (c u) -> p c u", u=2), turned[:].rearrange("p u c -> p c u"))
-            nc.vector.quantize_mx(out=h_words[e][:].bitcast(E4M3), scales=h_bytes[e][:], in_=h_flat)
+        def turn(experts, hs):
+            n = len(experts)
+            turned = psum.tile([P, n, 2, C], F32, name="turned")
+            for i, h in enumerate(hs):
+                for u in range(2):
+                    nc.tensor.transpose(turned[:, i, u, :], h[:].bitcast(F32)[:, u, :, 0], ident[:])
+            h_grp = work.tile([P, n * C * 4], BF16, name="h_grp", align_bytes=64)
+            nc.scalar.copy(
+                h_grp[:].bitcast(F32).rearrange("p (e c u) -> p e c u", e=n, u=2),
+                turned[:].rearrange("p e u c -> p e c u"),
+            )
+            words = keep.tile([P, n * C], U32, name=f"h_words{experts[0]}", align_bytes=64)
+            planes = keep.tile([P, n * C], U8, name=f"h_bytes{experts[0]}", align_bytes=64)
+            nc.vector.quantize_mx(out=words[:].bitcast(E4M3), scales=planes[:], in_=h_grp[:])
+            for i, e in enumerate(experts):
+                h_words[e], h_bytes[e] = words[:, C * i : C * (i + 1)], planes[:, C * i : C * (i + 1)]
 
         gate(0)
-        h0 = hidden(0)
-        gather_late(3, act_at)
         gate(1)
-        turn(0, h0)
+        h0 = hidden(0)
         h1 = hidden(1)
         gate(2)
-        turn(1, h1)
         gate(3)
-        load_scales(sc2, w2_scales)
+        turn((0, 1), (h0, h1))
+        load_scales(sc2, w2_scales, E)
         h2 = hidden(2)
         h3 = hidden(3)
-        turn(2, h2)
-        turn(3, h3)
+        turn((2,), (h2,))
+        turn((3,), (h3,))
 
-        copies = (nc.vector.tensor_copy, nc.scalar.copy)
-        for pair in range(2):
-            for half, queue in enumerate((nc.sync, nc.scalar)):
-                if pair == 0:
-                    y = psum1.tile([P, 2, C], F32, name=f"y_early{half}")
-                else:
-                    y = psum.tile([P, 2, C], F32, name=f"y_last{half}", tag="acc_a")
-                for i in range(2):
-                    e = 2 * pair + i
-                    nc.tensor.matmul_mx(
-                        out=y[:, i, :],
-                        lhsT=w2_t[:, e, 2 * P * half : 2 * P * (half + 1)].bitcast(E2M1),
-                        lhsT_scale=sc2[:, e, P * half : P * (half + 1)],
-                        rhs=h_words[e][:].bitcast(E4M3),
-                        rhs_scale=h_bytes[e][:],
-                        start=True,
-                        stop=True,
-                    )
-                copies[half](o_sb[half][:, :, 2 * pair : 2 * pair + 2, :], y[:].rearrange("p e (m u) -> p m e u", m=R))
-                if pair == 1:
-                    queue.dma_start(out[P * half : P * (half + 1), :], o_sb[half][:].rearrange("p m e u -> p (m e u)"))
+        def second(experts, half, y, copy):
+            for i, e in enumerate(experts):
+                nc.tensor.matmul_mx(
+                    out=y[:, i, :],
+                    lhsT=w2_t[:, e, 2 * P * half : 2 * P * (half + 1)].bitcast(E2M1),
+                    lhsT_scale=sc2[:, N * e + P * half : N * e + P * (half + 1)],
+                    rhs=h_words[e].bitcast(E4M3),
+                    rhs_scale=h_bytes[e],
+                    start=True,
+                    stop=True,
+                )
+            copy(o_sb[half][:, :, experts[0] : experts[-1] + 1, :], y[:].rearrange("p e (m u) -> p m e u", m=R))
+
+        for half in range(2):
+            second((0, 1), half, psum1.tile([P, 2, C], F32, name=f"y_early{half}"), nc.scalar.copy)
+        for e, tag in ((2, "acc_a"), (3, "acc_b")):
+            for half, copy in enumerate((nc.vector.tensor_copy, nc.scalar.copy)):
+                second((e,), half, psum.tile([P, 1, C], F32, name=f"y{e}{half}", tag=tag), copy)
+        for half in range(2):
+            (nc.sync, nc.scalar)[half].dma_start(
+                out[P * half : P * (half + 1), :], o_sb[half][:].rearrange("p m e u -> p (m e u)")
+            )

@@ -22,7 +22,7 @@ RELU = mybir.ActivationFunctionType.Relu
 MULT = mybir.AluOpType.mult
 
 KIB = 1024
-CHUNKS = ((0, 0, 160, 256), (0, 256, 416, 512), (1, 0, 128, 512), (2, 0, 0, 512))
+CHUNKS = ((0, 0, 320, 512), (1, 0, 64, 512), (2, 0, 96, 512))
 
 
 def tile_moe_eps_glu_relu_kernel(
@@ -42,18 +42,22 @@ def tile_moe_eps_glu_relu_kernel(
         offsets = keep.tile([P, E * C // 16], U16, name="offsets")
         x_words = [keep.tile([P, T], U32, name=f"x_words{s}", align_bytes=64) for s in range(PASSES)]
         x_bytes = [keep.tile([P, T], U8, name=f"x_bytes{s}", align_bytes=64) for s in range(PASSES)]
-        sc13 = [keep.tile([P, E * PASSES * H], U8, name=f"sc13_{m}", align_bytes=64) for m in range(2)]
-        sc2 = sc13[0][:, : E * N]
+        sc13 = {
+            (pair, m): keep.tile([P, 2 * PASSES * H], U8, name=f"sc13_{pair}{m}", align_bytes=64)
+            for pair in range(2)
+            for m in range(2)
+        }
+        sc2 = sc13[0, 0][:, : E * N]
         h_words, h_bytes = {}, {}
         act = [keep.tile([P, 2, P, 2], F32, name=f"act{e}") for e in range(E)]
         ident = keep.tile([P, P], F32, name="ident")
         o_sb = [keep.tile([P, R, E, C // R], F32, name=f"o_sb{half}") for half in range(2)]
 
-        for plane in (sc13[0], x_bytes[0], sc13[1], x_bytes[1], x_bytes[2]):
+        for plane in list(sc13.values()) + x_bytes:
             nc.vector.memset(plane[:].bitcast(I32), 0)
         make_identity(nc, ident[:])
 
-        raw_at = (0, 4, 8, 16)
+        raw_at = (0, 8, 16)
         grp_at = (24, 28, 32)
 
         nc.sync.dma_start(offsets[:], offs)
@@ -73,8 +77,8 @@ def tile_moe_eps_glu_relu_kernel(
             for i, (e, s) in enumerate((e, s) for e in experts for s in passes):
                 w13[e, m, s] = home[:, i, :]
 
-        for e in range(2):
-            load_w13(0, (e,), (0, 1), None)
+        for m, e in ((0, 0), (0, 1), (1, 0), (1, 1)):
+            load_w13(m, (e,), (0, 1), None)
 
         def load_scales(plane, scales, rows):
             src = scales.bitcast(I32).rearrange("e s (q r) c -> r q (e s) c", r=4)
@@ -82,8 +86,8 @@ def tile_moe_eps_glu_relu_kernel(
             for r in range(4):
                 nc.sync.dma_start(dst[r:P:32, :, :], src[r])
 
-        load_scales(sc13[0][:], w1_scales, E * PASSES)
-        load_scales(sc13[1][:], w3_scales, E * PASSES)
+        for (pair, m), plane in zip(sc13, sc13.values()):
+            load_scales(plane[:], (w1_scales, w3_scales)[m][2 * pair : 2 * pair + 2], 2 * PASSES)
 
         g_words, g_bytes = {}, {}
 
@@ -107,8 +111,7 @@ def tile_moe_eps_glu_relu_kernel(
             dst = x_grp[s][:, a:b].rearrange("p (c i) t -> p c t i", i=4)
             src = x_raw[i][:].rearrange("p t (c i) -> p c t i", i=4)
             cut = (v - a) // 4
-            if cut:
-                nc.vector.tensor_copy(dst[:, :cut], src[:, :cut])
+            nc.vector.tensor_copy(dst[:, :cut], src[:, :cut])
             nc.scalar.activation(dst[:, cut:], src[:, cut:], COPY)
             nc.vector.quantize_mx(
                 out=x_words[s][:, a:b].bitcast(E4M3),
@@ -117,18 +120,25 @@ def tile_moe_eps_glu_relu_kernel(
             )
             if b == T:
                 gather_kept(s, 0)
-                gather_kept(s, 1)
+                if s == 0:
+                    gather_kept(s, 1)
+        for s in (1, 2):
+            gather(
+                s,
+                (2, 3),
+                shared([P, 2 * C], U32, f"g_words{s}1", grp_at[2] + 2 * (s - 1)),
+                shared([P, 2 * C], U8, f"g_bytes{s}1", grp_at[2] + 2 * (s - 1) + 1),
+            )
 
-        load_w13(1, (0,), (0, 1), raw_at[0])
-        load_w13(1, (1,), (0, 1), raw_at[0] + 2)
-        load_w13(0, (0, 1), (2,), raw_at[1])
-        load_w13(1, (0, 1), (2,), raw_at[1] + 2)
-        load_w13(0, (2,), (0, 1, 2), raw_at[2])
-        load_w13(0, (3,), (0, 1, 2), raw_at[2] + 3)
-        load_w13(1, (2,), (0, 1, 2), raw_at[3])
-        load_w13(1, (3,), (0, 1), raw_at[3] + 3)
-        load_w13(1, (3,), (2,), raw_at[3] + 5)
-        w2_t = shared([P, E, 2 * N], U8, "w2_t", raw_at[3] + 6)
+        for e in range(2):
+            for m in range(2):
+                load_w13(m, (e,), (2,), raw_at[0] + 2 * e + m)
+        load_w13(0, (2,), (0, 1, 2), raw_at[1])
+        load_w13(1, (2,), (0, 1, 2), raw_at[1] + 3)
+        load_w13(0, (3,), (0, 1, 2), raw_at[2])
+        load_w13(1, (3,), (0, 1), raw_at[2] + 3)
+        load_w13(1, (3,), (2,), raw_at[2] + 5)
+        w2_t = shared([P, E, 2 * N], U8, "w2_t", raw_at[2] + 6)
         nc.sync.dma_start(w2_t[:].bitcast(I32), w2_words[:, 0].bitcast(I32).rearrange("e p c -> p e c"))
 
         def product(e, m, name):
@@ -139,7 +149,7 @@ def tile_moe_eps_glu_relu_kernel(
                     lhsT=g_words[s, e].bitcast(E4M3),
                     lhsT_scale=g_bytes[s, e],
                     rhs=w13[e, m, s].bitcast(E2M1),
-                    rhs_scale=sc13[m][:, H * (PASSES * e + s) : H * (PASSES * e + s + 1)],
+                    rhs_scale=sc13[e // 2, m][:, H * (PASSES * (e % 2) + s) : H * (PASSES * (e % 2) + s + 1)],
                     start=(s == 0),
                     stop=(s == PASSES - 1),
                 )
@@ -151,8 +161,9 @@ def tile_moe_eps_glu_relu_kernel(
         def gate(e):
             nc.scalar.activation(act[e][:], by_half(product(e, 0, "acc_a")), RELU)
 
-        def hidden(e):
-            h = work.tile([P, 2, P, 2], BF16, name="h")
+        def hidden(e, at=None):
+            shape = [P, 2, P, 2]
+            h = keep.tile(shape, BF16, name=f"h{e}") if at is None else shared(shape, BF16, f"h{e}", at)
             acc = by_half(product(e, 1, "acc_b"))
             for a, b in ((0, 1), (1, 2)) if e == E - 1 else ((0, 2),):
                 nc.vector.tensor_tensor(h[:, a:b], acc[:, a:b], act[e][:, a:b], MULT)
@@ -176,14 +187,14 @@ def tile_moe_eps_glu_relu_kernel(
                 h_words[e], h_bytes[e] = words[:, C * i : C * (i + 1)], planes[:, C * i : C * (i + 1)]
 
         gate(0)
-        gate(1)
         h0 = hidden(0)
+        gate(1)
+        load_scales(sc2, w2_scales, E)
         h1 = hidden(1)
+        turn((0, 1), (h0, h1))
         gate(2)
         gate(3)
-        turn((0, 1), (h0, h1))
-        load_scales(sc2, w2_scales, E)
-        h2 = hidden(2)
+        h2 = hidden(2, raw_at[2])
         h3 = hidden(3)
         turn((2,), (h2,))
         turn((3,), (h3,))

@@ -6,7 +6,8 @@ from concourse.masks import make_identity
 K, T, E, C, H, N = 1536, 512, 4, 128, 512, 256
 R = 4
 P = 128
-PASSES = K // 512
+PACK = 4
+PASSES = K // (P * PACK)
 FLOPS = E * (2 * 2 * K * C * H + 2 * H * C * N)
 
 F32 = mybir.dt.float32
@@ -21,8 +22,12 @@ COPY = mybir.ActivationFunctionType.Copy
 RELU = mybir.ActivationFunctionType.Relu
 MULT = mybir.AluOpType.mult
 
-KIB = 1024
-CHUNKS = ((0, 0, 320, 512), (1, 0, 64, 512), (2, 0, 96, 512))
+W1, W3 = 0, 1
+PAIRS = ((0, 1), (2, 3))
+PASS_BYTES = 2 * H
+X_BYTES = PACK * T * 4
+
+VECTOR_TOKENS = (320, 64, 0)
 
 
 def tile_moe_eps_glu_relu_kernel(
@@ -34,140 +39,114 @@ def tile_moe_eps_glu_relu_kernel(
         turns = ctx.enter_context(tc.tile_pool(name="turns", bufs=1))
         work = ctx.enter_context(tc.tile_pool(name="work", bufs=3))
         psum = ctx.enter_context(tc.psum_pool(name="psum", bufs=2))
-        psum1 = ctx.enter_context(tc.psum_pool(name="psum1", bufs=1))
+        psum_y = ctx.enter_context(tc.psum_pool(name="psum_y", bufs=1))
 
-        def shared(shape, dtype, name, kib):
-            return turns.tile(shape, dtype, name=name, align_bytes=64, offset=int(kib * KIB))
+        def place(shape, dtype, name, at):
+            if at is None:
+                return keep.tile(shape, dtype, name=name, align_bytes=64)
+            return turns.tile(shape, dtype, name=name, align_bytes=64, offset=at)
 
         offsets = keep.tile([P, E * C // 16], U16, name="offsets")
-        x_words = [keep.tile([P, T], U32, name=f"x_words{s}", align_bytes=64) for s in range(PASSES)]
-        x_bytes = [keep.tile([P, T], U8, name=f"x_bytes{s}", align_bytes=64) for s in range(PASSES)]
-        sc13 = {
-            (pair, m): keep.tile([P, 2 * PASSES * H], U8, name=f"sc13_{pair}{m}", align_bytes=64)
-            for pair in range(2)
-            for m in range(2)
+        x_words = [place([P, T], U32, f"x_words{s}", None) for s in range(PASSES)]
+        x_plane = [place([P, T], U8, f"x_plane{s}", None) for s in range(PASSES)]
+        w13_plane = {
+            (pair, m): place([P, 2 * PASSES * H], U8, f"w13_plane{pair}{m}", None) for pair in range(2) for m in (W1, W3)
         }
-        sc2 = sc13[0, 0][:, : E * N]
-        h_words, h_bytes = {}, {}
-        act = [keep.tile([P, 2, P, 2], F32, name=f"act{e}") for e in range(E)]
+        w2_plane = w13_plane[0, W1][:, : E * N]
+        gate = [keep.tile([P, 2, P, 2], F32, name=f"gate{e}") for e in range(E)]
         ident = keep.tile([P, P], F32, name="ident")
         o_sb = [keep.tile([P, R, E, C // R], F32, name=f"o_sb{half}") for half in range(2)]
 
-        for plane in list(sc13.values()) + x_bytes:
+        for plane in list(w13_plane.values()) + x_plane:
             nc.vector.memset(plane[:].bitcast(I32), 0)
         make_identity(nc, ident[:])
 
-        raw_at = (0, 8, 16)
-        grp_at = (24, 28, 32)
-
-        nc.sync.dma_start(offsets[:], offs)
         x_raw = []
-        for i, (s, a, v, b) in enumerate(CHUNKS):
-            raw = shared([P, 4, b - a], F32, f"x_raw{i}", raw_at[i])
-            nc.sync.dma_start(raw[:], xT[512 * s : 512 * (s + 1), a:b].rearrange("(p j) w -> p j w", j=4))
+        for s in range(PASSES):
+            raw = place([P, PACK, T], F32, f"x_raw{s}", s * X_BYTES)
+            nc.sync.dma_start(raw[:], xT[P * PACK * s : P * PACK * (s + 1), :].rearrange("(p t) w -> p t w", t=PACK))
             x_raw.append(raw)
+            if s == 0:
+                nc.sync.dma_start(offsets[:], offs)
 
-        w13 = {}
+        w13_words = {}
 
-        def load_w13(m, experts, passes, at):
-            shape, name = [P, len(experts) * len(passes), 2 * H], f"w13_{m}{experts[0]}{passes[0]}"
-            home = keep.tile(shape, U8, name=name, align_bytes=64) if at is None else shared(shape, U8, name, at)
-            words = (w1_words, w3_words)[m][experts[0] : experts[-1] + 1, passes[0] : passes[-1] + 1]
-            nc.sync.dma_start(home[:].bitcast(I32), words.bitcast(I32).rearrange("e s p c -> p (e s) c"))
+        def load_words(m, experts, passes, at):
+            home = place([P, len(experts) * len(passes), PASS_BYTES], U8, f"w13_words{m}{experts[0]}{passes[0]}", at)
+            rows = (w1_words, w3_words)[m][experts[0] : experts[-1] + 1, passes[0] : passes[-1] + 1]
+            nc.sync.dma_start(home[:].bitcast(I32), rows.bitcast(I32).rearrange("e s p c -> p (e s) c"))
             for i, (e, s) in enumerate((e, s) for e in experts for s in passes):
-                w13[e, m, s] = home[:, i, :]
+                w13_words[e, m, s] = home[:, i, :]
 
-        for m, e in ((0, 0), (0, 1), (1, 0), (1, 1)):
-            load_w13(m, (e,), (0, 1), None)
-
-        def load_scales(plane, scales, rows):
+        def load_scales(plane, scales, planes):
             src = scales.bitcast(I32).rearrange("e s (q r) c -> r q (e s) c", r=4)
-            dst = plane.bitcast(I32).rearrange("p (a c) -> p a c", a=rows)
+            dst = plane.bitcast(I32).rearrange("p (a c) -> p a c", a=planes)
             for r in range(4):
                 nc.sync.dma_start(dst[r:P:32, :, :], src[r])
 
-        for (pair, m), plane in zip(sc13, sc13.values()):
-            load_scales(plane[:], (w1_scales, w3_scales)[m][2 * pair : 2 * pair + 2], 2 * PASSES)
+        for m in (W1, W3):
+            for e in PAIRS[0]:
+                load_words(m, (e,), (0, 1), None)
+        for pair, m in w13_plane:
+            load_scales(w13_plane[pair, m][:], (w1_scales, w3_scales)[m][2 * pair : 2 * pair + 2], 2 * PASSES)
 
-        g_words, g_bytes = {}, {}
-
-        def gather(s, experts, words, planes):
-            lst = offsets[:, experts[0] * C // 16 : (experts[-1] + 1) * C // 16]
-            nc.vector.tensor_copy(words[:], x_words[s][:].indirect(lst))
-            nc.vector.tensor_copy(planes[:], x_bytes[s][:].indirect(lst))
-            for i, e in enumerate(experts):
-                g_words[s, e], g_bytes[s, e] = words[:, C * i : C * (i + 1)], planes[:, C * i : C * (i + 1)]
-
-        def gather_kept(s, pair):
-            gather(
-                s,
-                (2 * pair, 2 * pair + 1),
-                keep.tile([P, 2 * C], U32, name=f"g_words{s}{pair}", align_bytes=64),
-                keep.tile([P, 2 * C], U8, name=f"g_bytes{s}{pair}", align_bytes=64),
-            )
-
-        x_grp = [shared([P, T, 4], BF16, f"x_grp{s}", grp_at[s]) for s in range(PASSES)]
-        for i, (s, a, v, b) in enumerate(CHUNKS):
-            dst = x_grp[s][:, a:b].rearrange("p (c i) t -> p c t i", i=4)
-            src = x_raw[i][:].rearrange("p t (c i) -> p c t i", i=4)
-            cut = (v - a) // 4
-            nc.vector.tensor_copy(dst[:, :cut], src[:, :cut])
+        slot_words, slot_plane = {}, {}
+        x_grp = [place([P, T, PACK], BF16, f"x_grp{s}", None) for s in range(PASSES)]
+        for s in range(PASSES):
+            dst = x_grp[s][:].rearrange("p (c i) t -> p c t i", i=4)
+            src = x_raw[s][:].rearrange("p t (c i) -> p c t i", i=4)
+            cut = VECTOR_TOKENS[s] // 4
+            if cut:
+                nc.vector.tensor_copy(dst[:, :cut], src[:, :cut])
             nc.scalar.activation(dst[:, cut:], src[:, cut:], COPY)
             nc.vector.quantize_mx(
-                out=x_words[s][:, a:b].bitcast(E4M3),
-                scales=x_bytes[s][:, a:b],
-                in_=x_grp[s][:, a:b].rearrange("p c t -> p (c t)"),
+                out=x_words[s][:].bitcast(E4M3), scales=x_plane[s][:], in_=x_grp[s][:].rearrange("p c t -> p (c t)")
             )
-            if b == T:
-                gather_kept(s, 0)
-                if s == 0:
-                    gather_kept(s, 1)
-        for s in (1, 2):
-            gather(
-                s,
-                (2, 3),
-                shared([P, 2 * C], U32, f"g_words{s}1", grp_at[2] + 2 * (s - 1)),
-                shared([P, 2 * C], U8, f"g_bytes{s}1", grp_at[2] + 2 * (s - 1) + 1),
-            )
+            for pair, experts in enumerate(PAIRS):
+                entries = offsets[:, 2 * C * pair // 16 : 2 * C * (pair + 1) // 16]
+                words = place([P, 2 * C], U32, f"slot_words{s}{pair}", None)
+                plane = place([P, 2 * C], U8, f"slot_plane{s}{pair}", None)
+                nc.vector.tensor_copy(words[:], x_words[s][:].indirect(entries))
+                nc.vector.tensor_copy(plane[:], x_plane[s][:].indirect(entries))
+                for i, e in enumerate(experts):
+                    slot_words[s, e], slot_plane[s, e] = words[:, C * i : C * (i + 1)], plane[:, C * i : C * (i + 1)]
 
-        for e in range(2):
-            for m in range(2):
-                load_w13(m, (e,), (2,), raw_at[0] + 2 * e + m)
-        load_w13(0, (2,), (0, 1, 2), raw_at[1])
-        load_w13(1, (2,), (0, 1, 2), raw_at[1] + 3)
-        load_w13(0, (3,), (0, 1, 2), raw_at[2])
-        load_w13(1, (3,), (0, 1), raw_at[2] + 3)
-        load_w13(1, (3,), (2,), raw_at[2] + 5)
-        w2_t = shared([P, E, 2 * N], U8, "w2_t", raw_at[2] + 6)
+        late_w3_at = 2 * X_BYTES + PASSES * PASS_BYTES
+        for m in (W1, W3):
+            load_words(m, PAIRS[0], (2,), 2 * m * PASS_BYTES)
+        load_words(W1, (2,), (0, 1, 2), X_BYTES)
+        load_words(W1, (3,), (0, 1, 2), X_BYTES + PASSES * PASS_BYTES)
+        load_words(W3, (2,), (0, 1, 2), 2 * X_BYTES)
+        for s in range(PASSES):
+            load_words(W3, (3,), (s,), late_w3_at + s * PASS_BYTES)
+        w2_t = place([P, E, 2 * N], U8, "w2_t", late_w3_at + PASSES * PASS_BYTES)
         nc.sync.dma_start(w2_t[:].bitcast(I32), w2_words[:, 0].bitcast(I32).rearrange("e p c -> p e c"))
 
-        def product(e, m, name):
-            acc = psum.tile([P, H], F32, name=name)
+        def product(e, m):
+            acc = psum.tile([P, H], F32, name=("acc_a", "acc_b")[m])
             for s in range(PASSES):
+                first = H * (PASSES * (e % 2) + s)
                 nc.tensor.matmul_mx(
                     out=acc[:],
-                    lhsT=g_words[s, e].bitcast(E4M3),
-                    lhsT_scale=g_bytes[s, e],
-                    rhs=w13[e, m, s].bitcast(E2M1),
-                    rhs_scale=sc13[e // 2, m][:, H * (PASSES * (e % 2) + s) : H * (PASSES * (e % 2) + s + 1)],
+                    lhsT=slot_words[s, e].bitcast(E4M3),
+                    lhsT_scale=slot_plane[s, e],
+                    rhs=w13_words[e, m, s].bitcast(E2M1),
+                    rhs_scale=w13_plane[e // 2, m][:, first : first + H],
                     start=(s == 0),
                     stop=(s == PASSES - 1),
                 )
-            return acc
-
-        def by_half(acc):
             return acc[:].rearrange("p (q u d) -> p u q d", u=2, d=2)
 
-        def gate(e):
-            nc.scalar.activation(act[e][:], by_half(product(e, 0, "acc_a")), RELU)
+        def make_gate(e):
+            nc.scalar.activation(gate[e][:], product(e, W1), RELU)
 
-        def hidden(e, at=None):
-            shape = [P, 2, P, 2]
-            h = keep.tile(shape, BF16, name=f"h{e}") if at is None else shared(shape, BF16, f"h{e}", at)
-            acc = by_half(product(e, 1, "acc_b"))
-            for a, b in ((0, 1), (1, 2)) if e == E - 1 else ((0, 2),):
-                nc.vector.tensor_tensor(h[:, a:b], acc[:, a:b], act[e][:, a:b], MULT)
+        def hidden(e, b, at):
+            h = place([P, 2, P, 2], BF16, f"h{e}", at)
+            for u in (slice(0, 1), slice(1, 2)) if e == E - 1 else (slice(0, 2),):
+                nc.vector.tensor_tensor(h[:, u], b[:, u], gate[e][:, u], MULT)
             return h
+
+        h_words, h_plane = {}, {}
 
         def turn(experts, hs):
             n = len(experts)
@@ -175,49 +154,50 @@ def tile_moe_eps_glu_relu_kernel(
             for i, h in enumerate(hs):
                 for u in range(2):
                     nc.tensor.transpose(turned[:, i, u, :], h[:].bitcast(F32)[:, u, :, 0], ident[:])
-            h_grp = work.tile([P, n * C * 4], BF16, name="h_grp", align_bytes=64)
+            h_grp = work.tile([P, n * C * PACK], BF16, name="h_grp", align_bytes=64)
             nc.scalar.copy(
                 h_grp[:].bitcast(F32).rearrange("p (e c u) -> p e c u", e=n, u=2),
                 turned[:].rearrange("p e u c -> p e c u"),
             )
-            words = keep.tile([P, n * C], U32, name=f"h_words{experts[0]}", align_bytes=64)
-            planes = keep.tile([P, n * C], U8, name=f"h_bytes{experts[0]}", align_bytes=64)
-            nc.vector.quantize_mx(out=words[:].bitcast(E4M3), scales=planes[:], in_=h_grp[:])
+            words = place([P, n * C], U32, f"h_words{experts[0]}", None)
+            plane = place([P, n * C], U8, f"h_plane{experts[0]}", None)
+            nc.vector.quantize_mx(out=words[:].bitcast(E4M3), scales=plane[:], in_=h_grp[:])
             for i, e in enumerate(experts):
-                h_words[e], h_bytes[e] = words[:, C * i : C * (i + 1)], planes[:, C * i : C * (i + 1)]
+                h_words[e], h_plane[e] = words[:, C * i : C * (i + 1)], plane[:, C * i : C * (i + 1)]
 
-        gate(0)
-        h0 = hidden(0)
-        gate(1)
-        load_scales(sc2, w2_scales, E)
-        h1 = hidden(1)
-        turn((0, 1), (h0, h1))
-        gate(2)
-        gate(3)
-        h2 = hidden(2, raw_at[2])
-        h3 = hidden(3)
+        make_gate(0)
+        make_gate(1)
+        load_scales(w2_plane, w2_scales, E)
+        h0 = hidden(0, product(0, W3), None)
+        h1 = hidden(1, product(1, W3), None)
+        make_gate(2)
+        make_gate(3)
+        turn(PAIRS[0], (h0, h1))
+        b2 = product(2, W3)
+        b3 = product(3, W3)
+        h2 = hidden(2, b2, late_w3_at)
+        h3 = hidden(3, b3, None)
         turn((2,), (h2,))
         turn((3,), (h3,))
 
-        def second(experts, half, y, copy):
+        def second_layer(experts, half, y, copy):
             for i, e in enumerate(experts):
+                first = N * e + P * half
                 nc.tensor.matmul_mx(
                     out=y[:, i, :],
                     lhsT=w2_t[:, e, 2 * P * half : 2 * P * (half + 1)].bitcast(E2M1),
-                    lhsT_scale=sc2[:, N * e + P * half : N * e + P * (half + 1)],
+                    lhsT_scale=w2_plane[:, first : first + P],
                     rhs=h_words[e].bitcast(E4M3),
-                    rhs_scale=h_bytes[e],
+                    rhs_scale=h_plane[e],
                     start=True,
                     stop=True,
                 )
             copy(o_sb[half][:, :, experts[0] : experts[-1] + 1, :], y[:].rearrange("p e (m u) -> p m e u", m=R))
 
         for half in range(2):
-            second((0, 1), half, psum1.tile([P, 2, C], F32, name=f"y_early{half}"), nc.scalar.copy)
+            second_layer(PAIRS[0], half, psum_y.tile([P, 2, C], F32, name=f"y_first{half}"), nc.scalar.copy)
         for e, tag in ((2, "acc_a"), (3, "acc_b")):
             for half, copy in enumerate((nc.vector.tensor_copy, nc.scalar.copy)):
-                second((e,), half, psum.tile([P, 1, C], F32, name=f"y{e}{half}", tag=tag), copy)
-        for half in range(2):
-            (nc.sync, nc.scalar)[half].dma_start(
-                out[P * half : P * (half + 1), :], o_sb[half][:].rearrange("p m e u -> p (m e u)")
-            )
+                second_layer((e,), half, psum.tile([P, 1, C], F32, name=f"y{e}{half}", tag=tag), copy)
+        for half, queue in enumerate((nc.sync, nc.scalar)):
+            queue.dma_start(out[P * half : P * (half + 1), :], o_sb[half][:].rearrange("p m e u -> p (m e u)"))

@@ -38,8 +38,7 @@ def tile_moe_eps_glu_relu_kernel(
         keep = ctx.enter_context(tc.tile_pool(name="keep", bufs=1))
         turns = ctx.enter_context(tc.tile_pool(name="turns", bufs=1))
         work = ctx.enter_context(tc.tile_pool(name="work", bufs=3))
-        psum = ctx.enter_context(tc.psum_pool(name="psum", bufs=2))
-        psum_y = ctx.enter_context(tc.psum_pool(name="psum_y", bufs=1))
+        psum = ctx.enter_context(tc.psum_pool(name="psum", bufs=1))
 
         def place(shape, dtype, name, at):
             if at is None:
@@ -70,6 +69,9 @@ def tile_moe_eps_glu_relu_kernel(
                 nc.sync.dma_start(offsets[:], offs)
 
         w13_words = {}
+
+        def bank(number, shape, name):
+            return psum.tile(shape, F32, name=name, tag=f"bank{number}")
 
         def load_words(m, experts, passes, at):
             home = place([P, len(experts) * len(passes), PASS_BYTES], U8, f"w13_words{m}{experts[0]}{passes[0]}", at)
@@ -111,76 +113,98 @@ def tile_moe_eps_glu_relu_kernel(
                 for i, e in enumerate(experts):
                     slot_words[s, e], slot_plane[s, e] = words[:, C * i : C * (i + 1)], plane[:, C * i : C * (i + 1)]
 
-        late_w3_at = 2 * X_BYTES + PASSES * PASS_BYTES
         for m in (W1, W3):
-            load_words(m, PAIRS[0], (2,), 2 * m * PASS_BYTES)
-        load_words(W1, (2,), (0, 1, 2), X_BYTES)
-        load_words(W1, (3,), (0, 1, 2), X_BYTES + PASSES * PASS_BYTES)
-        load_words(W3, (2,), (0, 1, 2), 2 * X_BYTES)
-        for s in range(PASSES):
-            load_words(W3, (3,), (s,), late_w3_at + s * PASS_BYTES)
-        w2_t = place([P, E, 2 * N], U8, "w2_t", late_w3_at + PASSES * PASS_BYTES)
+            for e in PAIRS[0]:
+                load_words(m, (e,), (2,), (2 * m + e) * PASS_BYTES)
+        for m in (W1, W3):
+            for e in PAIRS[1]:
+                for s in range(PASSES):
+                    load_words(m, (e,), (s,), (1 + m) * X_BYTES + (PASSES * (e % 2) + s) * PASS_BYTES)
+        w2_t = place([P, E, 2 * N], U8, "w2_t", 2 * X_BYTES + 2 * PASSES * PASS_BYTES)
         nc.sync.dma_start(w2_t[:].bitcast(I32), w2_words[:, 0].bitcast(I32).rearrange("e p c -> p e c"))
 
-        def product(e, m):
-            acc = psum.tile([P, H], F32, name=("acc_a", "acc_b")[m])
+        def one_pass(acc, e, m, s, first, width):
+            at = H * (PASSES * (e % 2) + s) + first
+            nc.tensor.matmul_mx(
+                out=acc,
+                lhsT=slot_words[s, e].bitcast(E4M3),
+                lhsT_scale=slot_plane[s, e],
+                rhs=w13_words[e, m, s][:, 2 * first : 2 * (first + width)].bitcast(E2M1),
+                rhs_scale=w13_plane[e // 2, m][:, at : at + width],
+                start=(s == 0),
+                stop=(s == PASSES - 1),
+            )
+
+        def in_pairs(acc):
+            return acc.rearrange("p (q u d) -> p u q d", u=2, d=2)
+
+        def product(e, m, number):
+            acc = bank(number, [P, H], f"acc{e}{m}")
             for s in range(PASSES):
-                first = H * (PASSES * (e % 2) + s)
-                nc.tensor.matmul_mx(
-                    out=acc[:],
-                    lhsT=slot_words[s, e].bitcast(E4M3),
-                    lhsT_scale=slot_plane[s, e],
-                    rhs=w13_words[e, m, s].bitcast(E2M1),
-                    rhs_scale=w13_plane[e // 2, m][:, first : first + H],
-                    start=(s == 0),
-                    stop=(s == PASSES - 1),
-                )
-            return acc[:].rearrange("p (q u d) -> p u q d", u=2, d=2)
+                one_pass(acc[:], e, m, s, 0, H)
+            return in_pairs(acc[:])
 
-        def make_gate(e):
-            nc.scalar.activation(gate[e][:], product(e, W1), RELU)
+        def make_gate(e, number):
+            nc.scalar.activation(gate[e][:], product(e, W1, number), RELU)
 
-        def hidden(e, b, at):
-            h = place([P, 2, P, 2], BF16, f"h{e}", at)
-            for u in (slice(0, 1), slice(1, 2)) if e == E - 1 else (slice(0, 2),):
-                nc.vector.tensor_tensor(h[:, u], b[:, u], gate[e][:, u], MULT)
+        def hidden(e, b):
+            h = place([P, 2, P, 2], BF16, f"h{e}", None)
+            nc.vector.tensor_tensor(h[:], b, gate[e][:], MULT)
             return h
 
         h_words, h_plane = {}, {}
 
-        def turn(experts, hs):
+        def turn(h, room):
+            for u in range(2):
+                nc.tensor.transpose(room[:, C * u : C * (u + 1)], h[:].bitcast(F32)[:, u, :, 0], ident[:])
+
+        def quantise(experts, rooms):
             n = len(experts)
-            turned = psum.tile([P, n, 2, C], F32, name="turned")
-            for i, h in enumerate(hs):
-                for u in range(2):
-                    nc.tensor.transpose(turned[:, i, u, :], h[:].bitcast(F32)[:, u, :, 0], ident[:])
             h_grp = work.tile([P, n * C * PACK], BF16, name="h_grp", align_bytes=64)
-            nc.scalar.copy(
-                h_grp[:].bitcast(F32).rearrange("p (e c u) -> p e c u", e=n, u=2),
-                turned[:].rearrange("p e u c -> p e c u"),
-            )
+            for i, room in enumerate(rooms):
+                nc.scalar.copy(
+                    h_grp[:, i * C * PACK : (i + 1) * C * PACK].bitcast(F32).rearrange("p (c u) -> p c u", u=2),
+                    room.rearrange("p (u c) -> p c u", u=2),
+                )
             words = place([P, n * C], U32, f"h_words{experts[0]}", None)
             plane = place([P, n * C], U8, f"h_plane{experts[0]}", None)
             nc.vector.quantize_mx(out=words[:].bitcast(E4M3), scales=plane[:], in_=h_grp[:])
             for i, e in enumerate(experts):
                 h_words[e], h_plane[e] = words[:, C * i : C * (i + 1)], plane[:, C * i : C * (i + 1)]
 
-        make_gate(0)
-        make_gate(1)
+        make_gate(0, 0)
+        make_gate(1, 1)
         load_scales(w2_plane, w2_scales, E)
-        h0 = hidden(0, product(0, W3), None)
-        h1 = hidden(1, product(1, W3), None)
-        make_gate(2)
-        make_gate(3)
-        turn(PAIRS[0], (h0, h1))
-        b2 = product(2, W3)
-        b3 = product(3, W3)
-        h2 = hidden(2, b2, late_w3_at)
-        h3 = hidden(3, b3, None)
-        turn((2,), (h2,))
-        turn((3,), (h3,))
+        h0 = hidden(0, product(0, W3, 2))
+        h1 = hidden(1, product(1, W3, 3))
+        shared = [bank(0, [P, H], "shared_low"), bank(4, [P, H], "shared_high")]
+        for s in range(PASSES):
+            for side in range(2):
+                one_pass(shared[side][:, : H // 2], 2, W1, s, side * H // 2, H // 2)
+        for side, h in enumerate((h0, h1)):
+            turn(h, shared[side][:, H // 2 :])
+        for side in range(2):
+            q = slice(side * P // 2, (side + 1) * P // 2)
+            nc.scalar.activation(gate[2][:, :, q, :], in_pairs(shared[side][:, : H // 2]), RELU)
+        quantise(PAIRS[0], [shared[side][:, H // 2 :] for side in range(2)])
+        make_gate(3, 1)
+        h2 = hidden(2, product(2, W3, 2))
+        last = [bank(5, [P, H], "last_low"), bank(3, [P, H], "last_high")]
+        for s in range(PASSES):
+            for side in range(2):
+                one_pass(last[side][:, : H // 2], 3, W3, s, side * H // 2, H // 2)
+        h3 = place([P, 2, P, 2], BF16, "h3", None)
+        for side in range(2):
+            q = slice(side * P // 2, (side + 1) * P // 2)
+            nc.vector.tensor_tensor(h3[:, :, q, :], in_pairs(last[side][:, : H // 2]), gate[3][:, :, q, :], MULT)
+        turn(h2, last[0][:, H // 2 :])
+        quantise((2,), [last[0][:, H // 2 :]])
+        room = bank(6, [P, 2 * C], "turned3")
+        turn(h3, room[:])
+        quantise((3,), [room[:]])
 
-        def second_layer(experts, half, y, copy):
+        def second_layer(experts, half, number, copy):
+            y = bank(number, [P, len(experts), C], f"y{experts[0]}{half}")
             for i, e in enumerate(experts):
                 first = N * e + P * half
                 nc.tensor.matmul_mx(
@@ -194,10 +218,8 @@ def tile_moe_eps_glu_relu_kernel(
                 )
             copy(o_sb[half][:, :, experts[0] : experts[-1] + 1, :], y[:].rearrange("p e (m u) -> p m e u", m=R))
 
-        for half in range(2):
-            second_layer(PAIRS[0], half, psum_y.tile([P, 2, C], F32, name=f"y_first{half}"), nc.scalar.copy)
-        for e, tag in ((2, "acc_a"), (3, "acc_b")):
-            for half, copy in enumerate((nc.vector.tensor_copy, nc.scalar.copy)):
-                second_layer((e,), half, psum.tile([P, 1, C], F32, name=f"y{e}{half}", tag=tag), copy)
-        for half, queue in enumerate((nc.sync, nc.scalar)):
+        for experts, numbers in ((PAIRS[0], (7, 0)), ((2,), (1, 4)), ((3,), (2, 3))):
+            for half, copy in ((1, nc.scalar.copy), (0, nc.vector.tensor_copy)):
+                second_layer(experts, half, numbers[half], copy)
+        for half, queue in ((1, nc.sync), (0, nc.scalar)):
             queue.dma_start(out[P * half : P * (half + 1), :], o_sb[half][:].rearrange("p m e u -> p (m e u)"))

@@ -86,9 +86,9 @@ def tile_moe_eps_glu_relu_kernel(
             for r in range(4):
                 nc.sync.dma_start(dst[r:P:32, :, :], src[r])
 
-        for m in (W1, W3):
+        for m, passes in ((W1, (0, 1)), (W3, (0,))):
             for e in PAIRS[0]:
-                load_words(m, (e,), (0, 1), None)
+                load_words(m, (e,), passes, None)
         for pair, m in w13_plane:
             load_scales(w13_plane[pair, m][:], (w1_scales, w3_scales)[m][2 * pair : 2 * pair + 2], 2 * PASSES)
 
@@ -113,23 +113,30 @@ def tile_moe_eps_glu_relu_kernel(
                 for i, e in enumerate(experts):
                     slot_words[s, e], slot_plane[s, e] = words[:, C * i : C * (i + 1)], plane[:, C * i : C * (i + 1)]
 
-        for m in (W1, W3):
+        for i, (m, s) in enumerate(((W3, 1), (W1, 2), (W3, 2))):
             for e in PAIRS[0]:
-                load_words(m, (e,), (2,), (2 * m + e) * PASS_BYTES)
-        for m in (W1, W3):
-            for e in PAIRS[1]:
-                for s in range(PASSES):
-                    load_words(m, (e,), (s,), (1 + m) * X_BYTES + (PASSES * (e % 2) + s) * PASS_BYTES)
+                load_words(m, (e,), (s,), (2 * i + e) * PASS_BYTES)
+        for m, e, passes in ((W1, 2, PASSES), (W1, 3, PASSES), (W3, 2, PASSES), (W3, 3, 1)):
+            for s in range(passes):
+                load_words(m, (e,), (s,), (1 + m) * X_BYTES + (PASSES * (e % 2) + s) * PASS_BYTES)
+        last_words = []
+        for side in range(2):
+            at = 2 * X_BYTES + (PASSES + 1 + side) * PASS_BYTES
+            home = place([P, PASSES - 1, H], U8, f"last_words{side}", at)
+            rows = w3_words[E - 1, 1:].bitcast(I32).rearrange("s p c -> p s c")
+            nc.sync.dma_start(home[:].bitcast(I32), rows[:, :, side * H // 4 : (side + 1) * H // 4])
+            last_words.append(home)
         w2_t = place([P, E, 2 * N], U8, "w2_t", 2 * X_BYTES + 2 * PASSES * PASS_BYTES)
         nc.sync.dma_start(w2_t[:].bitcast(I32), w2_words[:, 0].bitcast(I32).rearrange("e p c -> p e c"))
 
-        def one_pass(acc, e, m, s, first, width):
+        def one_pass(acc, e, m, s, first, words):
+            width = words.shape[1] // 2
             at = H * (PASSES * (e % 2) + s) + first
             nc.tensor.matmul_mx(
                 out=acc,
                 lhsT=slot_words[s, e].bitcast(E4M3),
                 lhsT_scale=slot_plane[s, e],
-                rhs=w13_words[e, m, s][:, 2 * first : 2 * (first + width)].bitcast(E2M1),
+                rhs=words.bitcast(E2M1),
                 rhs_scale=w13_plane[e // 2, m][:, at : at + width],
                 start=(s == 0),
                 stop=(s == PASSES - 1),
@@ -141,7 +148,7 @@ def tile_moe_eps_glu_relu_kernel(
         def product(e, m, number):
             acc = bank(number, [P, H], f"acc{e}{m}")
             for s in range(PASSES):
-                one_pass(acc[:], e, m, s, 0, H)
+                one_pass(acc[:], e, m, s, 0, w13_words[e, m, s])
             return in_pairs(acc[:])
 
         def make_gate(e, number):
@@ -180,7 +187,8 @@ def tile_moe_eps_glu_relu_kernel(
         shared = [bank(0, [P, H], "shared_low"), bank(4, [P, H], "shared_high")]
         for s in range(PASSES):
             for side in range(2):
-                one_pass(shared[side][:, : H // 2], 2, W1, s, side * H // 2, H // 2)
+                words = w13_words[2, W1, s][:, side * H : (side + 1) * H]
+                one_pass(shared[side][:, : H // 2], 2, W1, s, side * H // 2, words)
         for side, h in enumerate((h0, h1)):
             turn(h, shared[side][:, H // 2 :])
         for side in range(2):
@@ -190,9 +198,11 @@ def tile_moe_eps_glu_relu_kernel(
         make_gate(3, 1)
         h2 = hidden(2, product(2, W3, 2))
         last = [bank(5, [P, H], "last_low"), bank(3, [P, H], "last_high")]
-        for s in range(PASSES):
-            for side in range(2):
-                one_pass(last[side][:, : H // 2], 3, W3, s, side * H // 2, H // 2)
+        for side in range(2):
+            one_pass(last[side][:, : H // 2], 3, W3, 0, side * H // 2, w13_words[3, W3, 0][:, side * H : (side + 1) * H])
+        for side in range(2):
+            for s in range(1, PASSES):
+                one_pass(last[side][:, : H // 2], 3, W3, s, side * H // 2, last_words[side][:, s - 1, :])
         h3 = place([P, 2, P, 2], BF16, "h3", None)
         for side in range(2):
             q = slice(side * P // 2, (side + 1) * P // 2)

@@ -25,7 +25,6 @@ MULT = mybir.AluOpType.mult
 W1, W3 = 0, 1
 PAIRS = ((0, 1), (2, 3))
 PASS_BYTES = 2 * H
-X_BYTES = PACK * T * 4
 
 VECTOR_TOKENS = (320, 64, 0)
 
@@ -36,33 +35,30 @@ def tile_moe_eps_glu_relu_kernel(
     nc = tc.nc
     with ExitStack() as ctx:
         keep = ctx.enter_context(tc.tile_pool(name="keep", bufs=1))
-        turns = ctx.enter_context(tc.tile_pool(name="turns", bufs=1))
         work = ctx.enter_context(tc.tile_pool(name="work", bufs=3))
         psum = ctx.enter_context(tc.psum_pool(name="psum", bufs=1))
 
-        def place(shape, dtype, name, at):
-            if at is None:
-                return keep.tile(shape, dtype, name=name, align_bytes=64)
-            return turns.tile(shape, dtype, name=name, align_bytes=64, offset=at)
+        def place(shape, dtype, name):
+            return keep.tile(shape, dtype, name=name, align_bytes=64)
 
         offsets = keep.tile([P, E * C // 16], U16, name="offsets")
-        x_words = [place([P, T], U32, f"x_words{s}", None) for s in range(PASSES)]
-        x_plane = [place([P, T], U8, f"x_plane{s}", None) for s in range(PASSES)]
+        x_words = [place([P, T], U32, f"x_words{s}") for s in range(PASSES)]
+        x_plane = [place([P, T], U8, f"x_plane{s}") for s in range(PASSES)]
         w13_plane = {
-            (pair, m): place([P, 2 * PASSES * H], U8, f"w13_plane{pair}{m}", None) for pair in range(2) for m in (W1, W3)
+            (pair, m): place([P, 2 * PASSES * H], U8, f"w13_plane{pair}{m}") for pair in range(2) for m in (W1, W3)
         }
-        w2_plane = w13_plane[0, W1][:, : E * N]
+        w2_plane = place([P, E * N], U8, "w2_plane")
         gate = [keep.tile([P, 2, P, 2], F32, name=f"gate{e}") for e in range(E)]
         ident = keep.tile([P, P], F32, name="ident")
         o_sb = [keep.tile([P, R, E, C // R], F32, name=f"o_sb{half}") for half in range(2)]
 
-        for plane in list(w13_plane.values()) + x_plane:
+        for plane in x_plane:
             nc.vector.memset(plane[:].bitcast(I32), 0)
         make_identity(nc, ident[:])
 
         x_raw = []
         for s in range(PASSES):
-            raw = place([P, PACK, T], F32, f"x_raw{s}", s * X_BYTES)
+            raw = place([P, PACK, T], F32, f"x_raw{s}")
             nc.sync.dma_start(raw[:], xT[P * PACK * s : P * PACK * (s + 1), :].rearrange("(p t) w -> p t w", t=PACK))
             x_raw.append(raw)
             if s == 0:
@@ -73,27 +69,42 @@ def tile_moe_eps_glu_relu_kernel(
         def bank(number, shape, name):
             return psum.tile(shape, F32, name=name, tag=f"bank{number}")
 
-        def load_words(m, experts, passes, at):
-            home = place([P, len(experts) * len(passes), PASS_BYTES], U8, f"w13_words{m}{experts[0]}{passes[0]}", at)
+        def load_words(m, experts, passes):
+            home = place([P, len(experts) * len(passes), PASS_BYTES], U8, f"w13_words{m}{experts[0]}{passes[0]}")
             rows = (w1_words, w3_words)[m][experts[0] : experts[-1] + 1, passes[0] : passes[-1] + 1]
             nc.sync.dma_start(home[:].bitcast(I32), rows.bitcast(I32).rearrange("e s p c -> p (e s) c"))
             for i, (e, s) in enumerate((e, s) for e in experts for s in passes):
                 w13_words[e, m, s] = home[:, i, :]
 
-        def load_scales(plane, scales, planes):
+        def load_scale_rows(plane, scales, planes, r):
             src = scales.bitcast(I32).rearrange("e s (q r) c -> r q (e s) c", r=4)
             dst = plane.bitcast(I32).rearrange("p (a c) -> p a c", a=planes)
-            for r in range(4):
-                nc.sync.dma_start(dst[r:P:32, :, :], src[r])
+            nc.sync.dma_start(dst[r:P:32, :, :], src[r])
 
-        for m, passes in ((W1, (0, 1)), (W3, (0,))):
-            for e in PAIRS[0]:
-                load_words(m, (e,), passes, None)
-        for pair, m in w13_plane:
-            load_scales(w13_plane[pair, m][:], (w1_scales, w3_scales)[m][2 * pair : 2 * pair + 2], 2 * PASSES)
+        wide = [(m, (e,), (0, 1)) for m in (W1, W3) for e in PAIRS[0]]
+        wide = wide + [(m, PAIRS[0], (2,)) for m in (W1, W3)] + [(W1, (e,), (0, 1, 2)) for e in PAIRS[1]]
+        narrow = [(pair, m, r) for pair in range(2) for m in (W1, W3) for r in range(4)]
+        for i, (m, experts, passes) in enumerate(wide):
+            for pair, which, r in narrow[2 * i : 2 * i + 2]:
+                scales = (w1_scales, w3_scales)[which][2 * pair : 2 * pair + 2]
+                load_scale_rows(w13_plane[pair, which][:], scales, 2 * PASSES, r)
+            load_words(m, experts, passes)
+        for e, passes in ((2, PASSES), (3, 1)):
+            for s in range(passes):
+                load_words(W3, (e,), (s,))
+        last_words = []
+        for side in range(2):
+            home = place([P, PASSES - 1, H], U8, f"last_words{side}")
+            rows = w3_words[E - 1, 1:].bitcast(I32).rearrange("s p c -> p s c")
+            nc.sync.dma_start(home[:].bitcast(I32), rows[:, :, side * H // 4 : (side + 1) * H // 4])
+            last_words.append(home)
+        w2_t = place([P, E, 2 * N], U8, "w2_t")
+        nc.sync.dma_start(w2_t[:].bitcast(I32), w2_words[:, 0].bitcast(I32).rearrange("e p c -> p e c"))
+        for r in range(4):
+            load_scale_rows(w2_plane[:], w2_scales, E, r)
 
         slot_words, slot_plane = {}, {}
-        x_grp = [place([P, T, PACK], BF16, f"x_grp{s}", None) for s in range(PASSES)]
+        x_grp = [place([P, T, PACK], BF16, f"x_grp{s}") for s in range(PASSES)]
         for s in range(PASSES):
             dst = x_grp[s][:].rearrange("p (c i) t -> p c t i", i=4)
             src = x_raw[s][:].rearrange("p t (c i) -> p c t i", i=4)
@@ -106,28 +117,12 @@ def tile_moe_eps_glu_relu_kernel(
             )
             for pair, experts in enumerate(PAIRS):
                 entries = offsets[:, 2 * C * pair // 16 : 2 * C * (pair + 1) // 16]
-                words = place([P, 2 * C], U32, f"slot_words{s}{pair}", None)
-                plane = place([P, 2 * C], U8, f"slot_plane{s}{pair}", None)
+                words = place([P, 2 * C], U32, f"slot_words{s}{pair}")
+                plane = place([P, 2 * C], U8, f"slot_plane{s}{pair}")
                 nc.vector.tensor_copy(words[:], x_words[s][:].indirect(entries))
                 nc.vector.tensor_copy(plane[:], x_plane[s][:].indirect(entries))
                 for i, e in enumerate(experts):
                     slot_words[s, e], slot_plane[s, e] = words[:, C * i : C * (i + 1)], plane[:, C * i : C * (i + 1)]
-
-        for i, (m, s) in enumerate(((W3, 1), (W1, 2), (W3, 2))):
-            for e in PAIRS[0]:
-                load_words(m, (e,), (s,), (2 * i + e) * PASS_BYTES)
-        for m, e, passes in ((W1, 2, PASSES), (W1, 3, PASSES), (W3, 2, PASSES), (W3, 3, 1)):
-            for s in range(passes):
-                load_words(m, (e,), (s,), (1 + m) * X_BYTES + (PASSES * (e % 2) + s) * PASS_BYTES)
-        last_words = []
-        for side in range(2):
-            at = 2 * X_BYTES + (PASSES + 1 + side) * PASS_BYTES
-            home = place([P, PASSES - 1, H], U8, f"last_words{side}", at)
-            rows = w3_words[E - 1, 1:].bitcast(I32).rearrange("s p c -> p s c")
-            nc.sync.dma_start(home[:].bitcast(I32), rows[:, :, side * H // 4 : (side + 1) * H // 4])
-            last_words.append(home)
-        w2_t = place([P, E, 2 * N], U8, "w2_t", 2 * X_BYTES + 2 * PASSES * PASS_BYTES)
-        nc.sync.dma_start(w2_t[:].bitcast(I32), w2_words[:, 0].bitcast(I32).rearrange("e p c -> p e c"))
 
         def one_pass(acc, e, m, s, first, words):
             width = words.shape[1] // 2
@@ -155,7 +150,7 @@ def tile_moe_eps_glu_relu_kernel(
             nc.scalar.activation(gate[e][:], product(e, W1, number), RELU)
 
         def hidden(e, b):
-            h = place([P, 2, P, 2], BF16, f"h{e}", None)
+            h = place([P, 2, P, 2], BF16, f"h{e}")
             nc.vector.tensor_tensor(h[:], b, gate[e][:], MULT)
             return h
 
@@ -173,15 +168,14 @@ def tile_moe_eps_glu_relu_kernel(
                     h_grp[:, i * C * PACK : (i + 1) * C * PACK].bitcast(F32).rearrange("p (c u) -> p c u", u=2),
                     room.rearrange("p (u c) -> p c u", u=2),
                 )
-            words = place([P, n * C], U32, f"h_words{experts[0]}", None)
-            plane = place([P, n * C], U8, f"h_plane{experts[0]}", None)
+            words = place([P, n * C], U32, f"h_words{experts[0]}")
+            plane = place([P, n * C], U8, f"h_plane{experts[0]}")
             nc.vector.quantize_mx(out=words[:].bitcast(E4M3), scales=plane[:], in_=h_grp[:])
             for i, e in enumerate(experts):
                 h_words[e], h_plane[e] = words[:, C * i : C * (i + 1)], plane[:, C * i : C * (i + 1)]
 
         make_gate(0, 0)
         make_gate(1, 1)
-        load_scales(w2_plane, w2_scales, E)
         h0 = hidden(0, product(0, W3, 2))
         h1 = hidden(1, product(1, W3, 3))
         shared = [bank(0, [P, H], "shared_low"), bank(4, [P, H], "shared_high")]
@@ -203,7 +197,7 @@ def tile_moe_eps_glu_relu_kernel(
         for side in range(2):
             for s in range(1, PASSES):
                 one_pass(last[side][:, : H // 2], 3, W3, s, side * H // 2, last_words[side][:, s - 1, :])
-        h3 = place([P, 2, P, 2], BF16, "h3", None)
+        h3 = place([P, 2, P, 2], BF16, "h3")
         for side in range(2):
             q = slice(side * P // 2, (side + 1) * P // 2)
             nc.vector.tensor_tensor(h3[:, :, q, :], in_pairs(last[side][:, : H // 2]), gate[3][:, :, q, :], MULT)

@@ -81,17 +81,23 @@ def tile_moe_eps_glu_relu_kernel(
             dst = plane.bitcast(I32).rearrange("p (a c) -> p a c", a=planes)
             nc.sync.dma_start(dst[r:P:32, :, :], src[r])
 
-        wide = [(m, (e,), (0, 1)) for m in (W1, W3) for e in PAIRS[0]]
-        wide = wide + [(m, PAIRS[0], (2,)) for m in (W1, W3)] + [(W1, (e,), (0, 1, 2)) for e in PAIRS[1]]
-        narrow = [(pair, m, r) for pair in range(2) for m in (W1, W3) for r in range(4)]
-        for i, (m, experts, passes) in enumerate(wide):
-            for pair, which, r in narrow[2 * i : 2 * i + 2]:
-                scales = (w1_scales, w3_scales)[which][2 * pair : 2 * pair + 2]
-                load_scale_rows(w13_plane[pair, which][:], scales, 2 * PASSES, r)
-            load_words(m, experts, passes)
-        for e, passes in ((2, PASSES), (3, 1)):
+        def load_scales(pair):
+            for m in (W1, W3):
+                for r in range(4):
+                    scales = (w1_scales, w3_scales)[m][2 * pair : 2 * pair + 2]
+                    load_scale_rows(w13_plane[pair, m][:], scales, 2 * PASSES, r)
+
+        for e in PAIRS[0]:
+            load_words(W1, (e,), (0, 1))
+        load_scales(0)
+        for e in PAIRS[0]:
+            load_words(W3, (e,), (0, 1))
+        for m in (W1, W3):
+            load_words(m, PAIRS[0], (2,))
+        load_scales(1)
+        for m, e, passes in ((W1, 2, PASSES), (W1, 3, PASSES), (W3, 2, PASSES), (W3, 3, 1)):
             for s in range(passes):
-                load_words(W3, (e,), (s,))
+                load_words(m, (e,), (s,))
         last_words = []
         for side in range(2):
             home = place([P, PASSES - 1, H], U8, f"last_words{side}")
@@ -178,17 +184,11 @@ def tile_moe_eps_glu_relu_kernel(
         make_gate(1, 1)
         h0 = hidden(0, product(0, W3, 2))
         h1 = hidden(1, product(1, W3, 3))
-        shared = [bank(0, [P, H], "shared_low"), bank(4, [P, H], "shared_high")]
-        for s in range(PASSES):
-            for side in range(2):
-                words = w13_words[2, W1, s][:, side * H : (side + 1) * H]
-                one_pass(shared[side][:, : H // 2], 2, W1, s, side * H // 2, words)
+        room = bank(4, [P, H], "turned01")
         for side, h in enumerate((h0, h1)):
-            turn(h, shared[side][:, H // 2 :])
-        for side in range(2):
-            q = slice(side * P // 2, (side + 1) * P // 2)
-            nc.scalar.activation(gate[2][:, :, q, :], in_pairs(shared[side][:, : H // 2]), RELU)
-        quantise(PAIRS[0], [shared[side][:, H // 2 :] for side in range(2)])
+            turn(h, room[:, side * H // 2 : (side + 1) * H // 2])
+        quantise(PAIRS[0], [room[:, side * H // 2 : (side + 1) * H // 2] for side in range(2)])
+        make_gate(2, 0)
         make_gate(3, 1)
         h2 = hidden(2, product(2, W3, 2))
         last = [bank(5, [P, H], "last_low"), bank(3, [P, H], "last_high")]

@@ -52,7 +52,7 @@ def tile_moe_eps_glu_relu_kernel(
         ident = keep.tile([P, P], F32, name="ident")
         o_sb = [keep.tile([P, R, E, C // R], F32, name=f"o_sb{half}") for half in range(2)]
 
-        for plane in x_plane:
+        for plane in list(w13_plane.values()) + x_plane + [w2_plane]:
             nc.vector.memset(plane[:].bitcast(I32), 0)
         make_identity(nc, ident[:])
 
@@ -92,10 +92,11 @@ def tile_moe_eps_glu_relu_kernel(
         load_scales(0)
         for e in PAIRS[0]:
             load_words(W3, (e,), (0, 1))
-        for m in (W1, W3):
-            load_words(m, PAIRS[0], (2,))
+        load_words(W1, PAIRS[0], (2,))
+        load_words(W1, (2,), (0, 1, 2))
+        load_words(W3, PAIRS[0], (2,))
         load_scales(1)
-        for m, e, passes in ((W1, 2, PASSES), (W1, 3, PASSES), (W3, 2, PASSES), (W3, 3, 1)):
+        for m, e, passes in ((W1, 3, PASSES), (W3, 2, PASSES), (W3, 3, 1)):
             for s in range(passes):
                 load_words(m, (e,), (s,))
         last_words = []
@@ -184,11 +185,17 @@ def tile_moe_eps_glu_relu_kernel(
         make_gate(1, 1)
         h0 = hidden(0, product(0, W3, 2))
         h1 = hidden(1, product(1, W3, 3))
-        room = bank(4, [P, H], "turned01")
+        shared = [bank(0, [P, H], "shared_low"), bank(4, [P, H], "shared_high")]
+        for s in range(PASSES):
+            for side in range(2):
+                words = w13_words[2, W1, s][:, side * H : (side + 1) * H]
+                one_pass(shared[side][:, : H // 2], 2, W1, s, side * H // 2, words)
         for side, h in enumerate((h0, h1)):
-            turn(h, room[:, side * H // 2 : (side + 1) * H // 2])
-        quantise(PAIRS[0], [room[:, side * H // 2 : (side + 1) * H // 2] for side in range(2)])
-        make_gate(2, 0)
+            turn(h, shared[side][:, H // 2 :])
+        for side in range(2):
+            q = slice(side * P // 2, (side + 1) * P // 2)
+            nc.scalar.activation(gate[2][:, :, q, :], in_pairs(shared[side][:, : H // 2]), RELU)
+        quantise(PAIRS[0], [shared[side][:, H // 2 :] for side in range(2)])
         make_gate(3, 1)
         h2 = hidden(2, product(2, W3, 2))
         last = [bank(5, [P, H], "last_low"), bank(3, [P, H], "last_high")]

@@ -35,7 +35,6 @@ def tile_moe_eps_glu_relu_kernel(
     nc = tc.nc
     with ExitStack() as ctx:
         keep = ctx.enter_context(tc.tile_pool(name="keep", bufs=1))
-        work = ctx.enter_context(tc.tile_pool(name="work", bufs=3))
         psum = ctx.enter_context(tc.psum_pool(name="psum", bufs=1))
 
         def place(shape, dtype, name):
@@ -96,7 +95,7 @@ def tile_moe_eps_glu_relu_kernel(
         load_words(W1, (2,), (0, 1, 2))
         load_words(W3, PAIRS[0], (2,))
         load_scales(1)
-        for m, e, passes in ((W1, 3, PASSES), (W3, 2, PASSES), (W3, 3, 1)):
+        for m, e, passes in ((W3, 2, PASSES), (W1, 3, PASSES), (W3, 3, 1)):
             for s in range(passes):
                 load_words(m, (e,), (s,))
         last_words = []
@@ -167,37 +166,43 @@ def tile_moe_eps_glu_relu_kernel(
             for u in range(2):
                 nc.tensor.transpose(room[:, C * u : C * (u + 1)], h[:].bitcast(F32)[:, u, :, 0], ident[:])
 
-        def quantise(experts, rooms):
+        def interleave(room, grp):
+            nc.scalar.copy(grp.bitcast(F32).rearrange("p (c u) -> p c u", u=2), room.rearrange("p (u c) -> p c u", u=2))
+
+        def quantise(experts, grp):
             n = len(experts)
-            h_grp = work.tile([P, n * C * PACK], BF16, name="h_grp", align_bytes=64)
-            for i, room in enumerate(rooms):
-                nc.scalar.copy(
-                    h_grp[:, i * C * PACK : (i + 1) * C * PACK].bitcast(F32).rearrange("p (c u) -> p c u", u=2),
-                    room.rearrange("p (u c) -> p c u", u=2),
-                )
             words = place([P, n * C], U32, f"h_words{experts[0]}")
             plane = place([P, n * C], U8, f"h_plane{experts[0]}")
-            nc.vector.quantize_mx(out=words[:].bitcast(E4M3), scales=plane[:], in_=h_grp[:])
+            nc.vector.quantize_mx(out=words[:].bitcast(E4M3), scales=plane[:], in_=grp)
             for i, e in enumerate(experts):
                 h_words[e], h_plane[e] = words[:, C * i : C * (i + 1)], plane[:, C * i : C * (i + 1)]
+
+        def hidden_half(h, e, side, acc):
+            q = slice(side * P // 2, (side + 1) * P // 2)
+            nc.vector.tensor_tensor(h[:, :, q, :], in_pairs(acc), gate[e][:, :, q, :], MULT)
 
         make_gate(0, 0)
         make_gate(1, 1)
         h0 = hidden(0, product(0, W3, 2))
         h1 = hidden(1, product(1, W3, 3))
-        shared = [bank(0, [P, H], "shared_low"), bank(4, [P, H], "shared_high")]
+        make_gate(2, 4)
+        shared = [bank(side, [P, H], f"shared{side}") for side in range(2)]
         for s in range(PASSES):
             for side in range(2):
-                words = w13_words[2, W1, s][:, side * H : (side + 1) * H]
-                one_pass(shared[side][:, : H // 2], 2, W1, s, side * H // 2, words)
+                words = w13_words[2, W3, s][:, side * H : (side + 1) * H]
+                one_pass(shared[side][:, : H // 2], 2, W3, s, side * H // 2, words)
         for side, h in enumerate((h0, h1)):
             turn(h, shared[side][:, H // 2 :])
+        h2 = place([P, 2, P, 2], BF16, "h2")
+        pair_grp = place([P, 2, C * PACK], BF16, "pair_grp")
+        for side in range(2):
+            hidden_half(h2, 2, side, shared[side][:, : H // 2])
+            interleave(shared[1 - side][:, H // 2 :], pair_grp[:, 1 - side, :])
+        quantise(PAIRS[0], pair_grp[:].rearrange("p e c -> p (e c)"))
+        last_a = product(3, W1, 2)
         for side in range(2):
             q = slice(side * P // 2, (side + 1) * P // 2)
-            nc.scalar.activation(gate[2][:, :, q, :], in_pairs(shared[side][:, : H // 2]), RELU)
-        quantise(PAIRS[0], [shared[side][:, H // 2 :] for side in range(2)])
-        make_gate(3, 1)
-        h2 = hidden(2, product(2, W3, 2))
+            nc.scalar.activation(gate[3][:, :, q, :], last_a[:, :, q, :], RELU)
         last = [bank(5, [P, H], "last_low"), bank(3, [P, H], "last_high")]
         for side in range(2):
             one_pass(last[side][:, : H // 2], 3, W3, 0, side * H // 2, w13_words[3, W3, 0][:, side * H : (side + 1) * H])
@@ -206,13 +211,12 @@ def tile_moe_eps_glu_relu_kernel(
                 one_pass(last[side][:, : H // 2], 3, W3, s, side * H // 2, last_words[side][:, s - 1, :])
         h3 = place([P, 2, P, 2], BF16, "h3")
         for side in range(2):
-            q = slice(side * P // 2, (side + 1) * P // 2)
-            nc.vector.tensor_tensor(h3[:, :, q, :], in_pairs(last[side][:, : H // 2]), gate[3][:, :, q, :], MULT)
-        turn(h2, last[0][:, H // 2 :])
-        quantise((2,), [last[0][:, H // 2 :]])
-        room = bank(6, [P, 2 * C], "turned3")
-        turn(h3, room[:])
-        quantise((3,), [room[:]])
+            hidden_half(h3, 3, side, last[side][:, : H // 2])
+        for e, h, room in ((2, h2, last[0][:, H // 2 :]), (3, h3, bank(6, [P, 2 * C], "turned3")[:])):
+            turn(h, room)
+            grp = place([P, C * PACK], BF16, f"h_grp{e}")
+            interleave(room, grp[:])
+            quantise((e,), grp[:])
 
         def second_layer(experts, half, number, copy):
             y = bank(number, [P, len(experts), C], f"y{experts[0]}{half}")
@@ -229,7 +233,7 @@ def tile_moe_eps_glu_relu_kernel(
                 )
             copy(o_sb[half][:, :, experts[0] : experts[-1] + 1, :], y[:].rearrange("p e (m u) -> p m e u", m=R))
 
-        for experts, numbers in ((PAIRS[0], (7, 0)), ((2,), (1, 4)), ((3,), (2, 3))):
+        for experts, numbers in ((PAIRS[0], (7, 4)), ((2,), (0, 1)), ((3,), (2, 3))):
             for half, copy in ((1, nc.scalar.copy), (0, nc.vector.tensor_copy)):
                 second_layer(experts, half, numbers[half], copy)
         for half, queue in ((1, nc.sync), (0, nc.scalar)):

@@ -89,11 +89,11 @@ def tile_moe_eps_glu_relu_kernel(
         for e in PAIRS[0]:
             load_words(W1, (e,), (0, 1))
         load_scales(0)
+        load_words(W1, (2,), (0, 1, 2))
         for e in PAIRS[0]:
             load_words(W3, (e,), (0, 1))
-        load_words(W1, PAIRS[0], (2,))
-        load_words(W1, (2,), (0, 1, 2))
-        load_words(W3, PAIRS[0], (2,))
+        for m in (W1, W3):
+            load_words(m, PAIRS[0], (2,))
         load_scales(1)
         for m, e, passes in ((W3, 2, PASSES), (W1, 3, PASSES), (W3, 3, 1)):
             for s in range(passes):

@@ -38,7 +38,7 @@ def tile_moe_eps_glu_relu_kernel(
         psum = ctx.enter_context(tc.psum_pool(name="psum", bufs=1))
 
         def place(shape, dtype, name):
-            return keep.tile(shape, dtype, name=name, align_bytes=64)
+            return keep.tile(shape, dtype, name=name, align_bytes=256)
 
         offsets = keep.tile([P, E * C // 16], U16, name="offsets")
         x_words = [place([P, T], U32, f"x_words{s}") for s in range(PASSES)]
@@ -47,9 +47,9 @@ def tile_moe_eps_glu_relu_kernel(
             (pair, m): place([P, 2 * PASSES * H], U8, f"w13_plane{pair}{m}") for pair in range(2) for m in (W1, W3)
         }
         w2_plane = place([P, E * N], U8, "w2_plane")
-        gate = [keep.tile([P, 2, P, 2], F32, name=f"gate{e}") for e in range(E)]
-        ident = keep.tile([P, P], F32, name="ident")
-        o_sb = [keep.tile([P, R, E, C // R], F32, name=f"o_sb{half}") for half in range(2)]
+        gate = [place([P, 2, P, 2], F32, f"gate{e}") for e in range(E)]
+        ident = place([P, P], F32, "ident")
+        o_sb = [place([P, R, E, C // R], F32, f"o_sb{half}") for half in range(2)]
 
         for plane in list(w13_plane.values()) + x_plane + [w2_plane]:
             nc.vector.memset(plane[:].bitcast(I32), 0)

@@ -26,7 +26,8 @@ W1, W3 = 0, 1
 PAIRS = ((0, 1), (2, 3))
 PASS_BYTES = 2 * H
 
-VECTOR_TOKENS = (320, 64, 0)
+HALF = T // 2
+VECTOR_TOKENS = ((HALF, 160), (0, 0), (0, 0))
 
 
 def tile_moe_eps_glu_relu_kernel(
@@ -57,9 +58,10 @@ def tile_moe_eps_glu_relu_kernel(
 
         x_raw = []
         for s in range(PASSES):
-            raw = place([P, PACK, T], F32, f"x_raw{s}")
-            nc.sync.dma_start(raw[:], xT[P * PACK * s : P * PACK * (s + 1), :].rearrange("(p t) w -> p t w", t=PACK))
-            x_raw.append(raw)
+            rows = xT[P * PACK * s : P * PACK * (s + 1), :].rearrange("(p t) w -> p t w", t=PACK)
+            x_raw.append([place([P, PACK, HALF], F32, f"x_raw{s}{side}") for side in range(2)])
+            for side in range(2):
+                nc.sync.dma_start(x_raw[s][side][:], rows[:, :, HALF * side : HALF * (side + 1)])
             if s == 0:
                 nc.sync.dma_start(offsets[:], offs)
 
@@ -68,12 +70,13 @@ def tile_moe_eps_glu_relu_kernel(
         def bank(number, shape, name):
             return psum.tile(shape, F32, name=name, tag=f"bank{number}")
 
-        def load_words(m, experts, passes):
-            home = place([P, len(experts) * len(passes), PASS_BYTES], U8, f"w13_words{m}{experts[0]}{passes[0]}")
-            rows = (w1_words, w3_words)[m][experts[0] : experts[-1] + 1, passes[0] : passes[-1] + 1]
-            nc.sync.dma_start(home[:].bitcast(I32), rows.bitcast(I32).rearrange("e s p c -> p (e s) c"))
-            for i, (e, s) in enumerate((e, s) for e in experts for s in passes):
-                w13_words[e, m, s] = home[:, i, :]
+        def load_words(m, first, last):
+            begin, end = PASSES * first[0] + first[1], PASSES * last[0] + last[1] + 1
+            home = place([P, end - begin, PASS_BYTES], U8, f"w13_words{m}{begin}")
+            rows = (w1_words, w3_words)[m].bitcast(I32).rearrange("e s p c -> p (e s) c")
+            nc.sync.dma_start(home[:].bitcast(I32), rows[:, begin:end, :])
+            for i in range(begin, end):
+                w13_words[i // PASSES, m, i % PASSES] = home[:, i - begin, :]
 
         def load_scale_rows(plane, scales, planes, r):
             src = scales.bitcast(I32).rearrange("e s (q r) c -> r q (e s) c", r=4)
@@ -86,18 +89,17 @@ def tile_moe_eps_glu_relu_kernel(
                     scales = (w1_scales, w3_scales)[m][2 * pair : 2 * pair + 2]
                     load_scale_rows(w13_plane[pair, m][:], scales, 2 * PASSES, r)
 
-        for e in PAIRS[0]:
-            load_words(W1, (e,), (0, 1))
-        load_scales(0)
-        load_words(W1, (2,), (0, 1, 2))
-        for e in PAIRS[0]:
-            load_words(W3, (e,), (0, 1))
         for m in (W1, W3):
-            load_words(m, PAIRS[0], (2,))
+            load_words(m, (0, 0), (0, 1))
+        load_scales(0)
+        for m in (W1, W3):
+            load_words(m, (0, 2), (1, 2))
+        load_words(W1, (2, 0), (2, 2))
         load_scales(1)
-        for m, e, passes in ((W3, 2, PASSES), (W1, 3, PASSES), (W3, 3, 1)):
-            for s in range(passes):
-                load_words(m, (e,), (s,))
+        load_words(W3, (2, 0), (2, 2))
+        load_words(W1, (3, 0), (3, 1))
+        load_words(W1, (3, 2), (3, 2))
+        load_words(W3, (3, 0), (3, 0))
         last_words = []
         for side in range(2):
             home = place([P, PASSES - 1, H], U8, f"last_words{side}")
@@ -110,17 +112,22 @@ def tile_moe_eps_glu_relu_kernel(
             load_scale_rows(w2_plane[:], w2_scales, E, r)
 
         slot_words, slot_plane = {}, {}
-        x_grp = [place([P, T, PACK], BF16, f"x_grp{s}") for s in range(PASSES)]
         for s in range(PASSES):
-            dst = x_grp[s][:].rearrange("p (c i) t -> p c t i", i=4)
-            src = x_raw[s][:].rearrange("p t (c i) -> p c t i", i=4)
-            cut = VECTOR_TOKENS[s] // 4
-            if cut:
-                nc.vector.tensor_copy(dst[:, :cut], src[:, :cut])
-            nc.scalar.activation(dst[:, cut:], src[:, cut:], COPY)
-            nc.vector.quantize_mx(
-                out=x_words[s][:].bitcast(E4M3), scales=x_plane[s][:], in_=x_grp[s][:].rearrange("p c t -> p (c t)")
-            )
+            for side in range(2):
+                grp = place([P, HALF, PACK], BF16, f"x_grp{s}{side}")
+                dst = grp[:].rearrange("p (c i) t -> p c t i", i=4)
+                src = x_raw[s][side][:].rearrange("p t (c i) -> p c t i", i=4)
+                cut = VECTOR_TOKENS[s][side] // 4
+                if cut:
+                    nc.vector.tensor_copy(dst[:, :cut], src[:, :cut])
+                if cut < HALF // 4:
+                    nc.scalar.activation(dst[:, cut:], src[:, cut:], COPY)
+                tokens = slice(HALF * side, HALF * (side + 1))
+                nc.vector.quantize_mx(
+                    out=x_words[s][:, tokens].bitcast(E4M3),
+                    scales=x_plane[s][:, tokens],
+                    in_=grp[:].rearrange("p c t -> p (c t)"),
+                )
             for pair, experts in enumerate(PAIRS):
                 entries = offsets[:, 2 * C * pair // 16 : 2 * C * (pair + 1) // 16]
                 words = place([P, 2 * C], U32, f"slot_words{s}{pair}")
@@ -152,9 +159,6 @@ def tile_moe_eps_glu_relu_kernel(
                 one_pass(acc[:], e, m, s, 0, w13_words[e, m, s])
             return in_pairs(acc[:])
 
-        def make_gate(e, number):
-            nc.scalar.activation(gate[e][:], product(e, W1, number), RELU)
-
         def hidden(e, b):
             h = place([P, 2, P, 2], BF16, f"h{e}")
             nc.vector.tensor_tensor(h[:], b, gate[e][:], MULT)
@@ -181,23 +185,29 @@ def tile_moe_eps_glu_relu_kernel(
             q = slice(side * P // 2, (side + 1) * P // 2)
             nc.vector.tensor_tensor(h[:, :, q, :], in_pairs(acc), gate[e][:, :, q, :], MULT)
 
-        make_gate(0, 0)
-        make_gate(1, 1)
-        h0 = hidden(0, product(0, W3, 2))
-        h1 = hidden(1, product(1, W3, 3))
-        make_gate(2, 4)
+        acc = {(e, m): bank(2 * m + e, [P, H], f"acc{e}{m}") for e in PAIRS[0] for m in (W1, W3)}
+        order = [(0, m, s) for m in (W1, W3) for s in (0, 1)]
+        order = order + [(1, W1, 0), (1, W1, 1), (0, W1, 2), (1, W1, 2), (0, W3, 2)] + [(1, W3, s) for s in range(PASSES)]
+        for e, m, s in order:
+            one_pass(acc[e, m][:], e, m, s, 0, w13_words[e, m, s])
+        for e in PAIRS[0]:
+            nc.scalar.activation(gate[e][:], in_pairs(acc[e, W1][:]), RELU)
+        h0 = hidden(0, in_pairs(acc[0, W3][:]))
+        h1 = hidden(1, in_pairs(acc[1, W3][:]))
         shared = [bank(side, [P, H], f"shared{side}") for side in range(2)]
         for s in range(PASSES):
             for side in range(2):
-                words = w13_words[2, W3, s][:, side * H : (side + 1) * H]
-                one_pass(shared[side][:, : H // 2], 2, W3, s, side * H // 2, words)
+                words = w13_words[2, W1, s][:, side * H : (side + 1) * H]
+                one_pass(shared[side][:, : H // 2], 2, W1, s, side * H // 2, words)
         for side, h in enumerate((h0, h1)):
             turn(h, shared[side][:, H // 2 :])
-        h2 = place([P, 2, P, 2], BF16, "h2")
+        for side in range(2):
+            q = slice(side * P // 2, (side + 1) * P // 2)
+            nc.scalar.activation(gate[2][:, :, q, :], in_pairs(shared[side][:, : H // 2]), RELU)
         pair_grp = place([P, 2, C * PACK], BF16, "pair_grp")
         for side in range(2):
-            hidden_half(h2, 2, side, shared[side][:, : H // 2])
-            interleave(shared[1 - side][:, H // 2 :], pair_grp[:, 1 - side, :])
+            interleave(shared[side][:, H // 2 :], pair_grp[:, side, :])
+        h2 = hidden(2, product(2, W3, 4))
         quantise(PAIRS[0], pair_grp[:].rearrange("p e c -> p (e c)"))
         last_a = product(3, W1, 2)
         for side in range(2):

@@ -26,8 +26,7 @@ W1, W3 = 0, 1
 PAIRS = ((0, 1), (2, 3))
 PASS_BYTES = 2 * H
 
-HALF = T // 2
-VECTOR_TOKENS = ((HALF, 160), (0, 0), (0, 0))
+VECTOR_TOKENS = (320, 128, 0)
 
 
 def tile_moe_eps_glu_relu_kernel(
@@ -38,8 +37,8 @@ def tile_moe_eps_glu_relu_kernel(
         keep = ctx.enter_context(tc.tile_pool(name="keep", bufs=1))
         psum = ctx.enter_context(tc.psum_pool(name="psum", bufs=1))
 
-        def place(shape, dtype, name):
-            return keep.tile(shape, dtype, name=name, align_bytes=256)
+        def place(shape, dtype, name, on=None):
+            return keep.tile(shape, dtype, name=name, tag=on or name, align_bytes=256)
 
         offsets = keep.tile([P, E * C // 16], U16, name="offsets")
         x_words = [place([P, T], U32, f"x_words{s}") for s in range(PASSES)]
@@ -58,10 +57,9 @@ def tile_moe_eps_glu_relu_kernel(
 
         x_raw = []
         for s in range(PASSES):
-            rows = xT[P * PACK * s : P * PACK * (s + 1), :].rearrange("(p t) w -> p t w", t=PACK)
-            x_raw.append([place([P, PACK, HALF], F32, f"x_raw{s}{side}") for side in range(2)])
-            for side in range(2):
-                nc.sync.dma_start(x_raw[s][side][:], rows[:, :, HALF * side : HALF * (side + 1)])
+            raw = place([P, PACK, T], F32, f"x_raw{s}")
+            nc.sync.dma_start(raw[:], xT[P * PACK * s : P * PACK * (s + 1), :].rearrange("(p t) w -> p t w", t=PACK))
+            x_raw.append(raw)
             if s == 0:
                 nc.sync.dma_start(offsets[:], offs)
 
@@ -96,9 +94,9 @@ def tile_moe_eps_glu_relu_kernel(
             load_words(m, (0, 2), (1, 2))
         load_words(W1, (2, 0), (2, 2))
         load_scales(1)
-        load_words(W3, (2, 0), (2, 2))
-        load_words(W1, (3, 0), (3, 1))
-        load_words(W1, (3, 2), (3, 2))
+        for m, e in ((W3, 2), (W1, 3)):
+            load_words(m, (e, 0), (e, 1))
+            load_words(m, (e, 2), (e, 2))
         load_words(W3, (3, 0), (3, 0))
         last_words = []
         for side in range(2):
@@ -112,30 +110,36 @@ def tile_moe_eps_glu_relu_kernel(
             load_scale_rows(w2_plane[:], w2_scales, E, r)
 
         slot_words, slot_plane = {}, {}
+
+        def gather(made, window, dtype, s, experts, on=None):
+            entries = offsets[:, C * experts[0] // 16 : C * (experts[-1] + 1) // 16]
+            home = place([P, len(experts) * C], dtype, f"slots{made is slot_words}{s}{experts[0]}", on)
+            nc.vector.tensor_copy(home[:], window[s][:].indirect(entries))
+            for i, e in enumerate(experts):
+                made[s, e] = home[:, C * i : C * (i + 1)]
+
         for s in range(PASSES):
-            for side in range(2):
-                grp = place([P, HALF, PACK], BF16, f"x_grp{s}{side}")
-                dst = grp[:].rearrange("p (c i) t -> p c t i", i=4)
-                src = x_raw[s][side][:].rearrange("p t (c i) -> p c t i", i=4)
-                cut = VECTOR_TOKENS[s][side] // 4
-                if cut:
-                    nc.vector.tensor_copy(dst[:, :cut], src[:, :cut])
-                if cut < HALF // 4:
-                    nc.scalar.activation(dst[:, cut:], src[:, cut:], COPY)
-                tokens = slice(HALF * side, HALF * (side + 1))
-                nc.vector.quantize_mx(
-                    out=x_words[s][:, tokens].bitcast(E4M3),
-                    scales=x_plane[s][:, tokens],
-                    in_=grp[:].rearrange("p c t -> p (c t)"),
-                )
-            for pair, experts in enumerate(PAIRS):
-                entries = offsets[:, 2 * C * pair // 16 : 2 * C * (pair + 1) // 16]
-                words = place([P, 2 * C], U32, f"slot_words{s}{pair}")
-                plane = place([P, 2 * C], U8, f"slot_plane{s}{pair}")
-                nc.vector.tensor_copy(words[:], x_words[s][:].indirect(entries))
-                nc.vector.tensor_copy(plane[:], x_plane[s][:].indirect(entries))
-                for i, e in enumerate(experts):
-                    slot_words[s, e], slot_plane[s, e] = words[:, C * i : C * (i + 1)], plane[:, C * i : C * (i + 1)]
+            grp = place([P, T, PACK], BF16, f"x_grp{s}")
+            dst = grp[:].rearrange("p (c i) t -> p c t i", i=4)
+            src = x_raw[s][:].rearrange("p t (c i) -> p c t i", i=4)
+            cut = VECTOR_TOKENS[s] // 4
+            if cut:
+                nc.vector.tensor_copy(dst[:, :cut], src[:, :cut])
+            nc.scalar.activation(dst[:, cut:], src[:, cut:], COPY)
+            nc.vector.quantize_mx(
+                out=x_words[s][:].bitcast(E4M3), scales=x_plane[s][:], in_=grp[:].rearrange("p c t -> p (c t)")
+            )
+            if s == 1:
+                gather(slot_plane, x_plane, U8, 0, PAIRS[1], on="x_raw1")
+            if s == 2:
+                gather(slot_words, x_words, U32, 1, PAIRS[1], on="x_raw2")
+            gather(slot_words, x_words, U32, s, PAIRS[0])
+            gather(slot_plane, x_plane, U8, s, PAIRS[0])
+            if s == 0:
+                gather(slot_words, x_words, U32, 0, PAIRS[1])
+        gather(slot_plane, x_plane, U8, 1, PAIRS[1], on="x_grp2")
+        gather(slot_words, x_words, U32, PASSES - 1, (2,))
+        gather(slot_plane, x_plane, U8, PASSES - 1, (2,))
 
         def one_pass(acc, e, m, s, first, words):
             width = words.shape[1] // 2
@@ -194,6 +198,8 @@ def tile_moe_eps_glu_relu_kernel(
             nc.scalar.activation(gate[e][:], in_pairs(acc[e, W1][:]), RELU)
         h0 = hidden(0, in_pairs(acc[0, W3][:]))
         h1 = hidden(1, in_pairs(acc[1, W3][:]))
+        gather(slot_words, x_words, U32, PASSES - 1, (3,), on="gate0")
+        gather(slot_plane, x_plane, U8, PASSES - 1, (3,), on="gate1")
         shared = [bank(side, [P, H], f"shared{side}") for side in range(2)]
         for s in range(PASSES):
             for side in range(2):

@@ -252,5 +252,5 @@ def tile_moe_eps_glu_relu_kernel(
         for experts, numbers in ((PAIRS[0], (7, 4)), ((2,), (0, 1)), ((3,), (2, 3))):
             for half, copy in ((1, nc.scalar.copy), (0, nc.vector.tensor_copy)):
                 second_layer(experts, half, numbers[half], copy)
-        for half, queue in ((1, nc.sync), (0, nc.scalar)):
-            queue.dma_start(out[P * half : P * (half + 1), :], o_sb[half][:].rearrange("p m e u -> p (m e u)"))
+        for half in (1, 0):
+            nc.sync.dma_start(out[P * half : P * (half + 1), :], o_sb[half][:].rearrange("p m e u -> p (m e u)"))

from contextlib import ExitStack

import concourse.mybir as mybir
from concourse.masks import make_identity

K, T, E, C, H, N = 1536, 512, 4, 128, 512, 256
R = 4
P = 128
PACK = 4
PASSES = K // (P * PACK)
FLOPS = E * (2 * 2 * K * C * H + 2 * H * C * N)

F32 = mybir.dt.float32
BF16 = mybir.dt.bfloat16
U32 = mybir.dt.uint32
I32 = mybir.dt.int32
U16 = mybir.dt.uint16
U8 = mybir.dt.uint8
E4M3 = mybir.dt.float8_e4m3fn_x4
E2M1 = mybir.dt.float4_e2m1fn_x4
COPY = mybir.ActivationFunctionType.Copy
RELU = mybir.ActivationFunctionType.Relu
MULT = mybir.AluOpType.mult

W1, W3 = 0, 1
PAIRS = ((0, 1), (2, 3))
PASS_BYTES = 2 * H

VECTOR_TOKENS = (320, 128, 0)


def tile_moe_eps_glu_relu_kernel(
    tc, xT, w1_words, w1_scales, w3_words, w3_scales, w2_words, w2_scales, offs, out
):
    nc = tc.nc
    with ExitStack() as ctx:
        keep = ctx.enter_context(tc.tile_pool(name="keep", bufs=1))
        psum = ctx.enter_context(tc.psum_pool(name="psum", bufs=1))

        def place(shape, dtype, name, on=None):
            return keep.tile(shape, dtype, name=name, tag=on or name, align_bytes=256)

        offsets = keep.tile([P, E * C // 16], U16, name="offsets")
        x_words = [place([P, T], U32, f"x_words{s}") for s in range(PASSES)]
        x_plane = [place([P, T], U8, f"x_plane{s}") for s in range(PASSES)]
        w13_plane = {
            (pair, m): place([P, 2 * PASSES * H], U8, f"w13_plane{pair}{m}") for pair in range(2) for m in (W1, W3)
        }
        w2_plane = place([P, E * N], U8, "w2_plane")
        gate = [place([P, 2, P, 2], F32, f"gate{e}") for e in range(E)]
        ident = place([P, P], F32, "ident")
        o_sb = [place([P, R, E, C // R], F32, f"o_sb{half}") for half in range(2)]

        for plane in list(w13_plane.values()) + x_plane + [w2_plane]:
            nc.vector.memset(plane[:].bitcast(I32), 0)
        make_identity(nc, ident[:])

        x_raw = []
        for s in range(PASSES):
            raw = place([P, PACK, T], F32, f"x_raw{s}")
            nc.sync.dma_start(raw[:], xT[P * PACK * s : P * PACK * (s + 1), :].rearrange("(p t) w -> p t w", t=PACK))
            x_raw.append(raw)
            if s == 0:
                nc.sync.dma_start(offsets[:], offs)

        w13_words = {}

        def bank(number, shape, name):
            return psum.tile(shape, F32, name=name, tag=f"bank{number}")

        def load_words(m, first, last):
            begin, end = PASSES * first[0] + first[1], PASSES * last[0] + last[1] + 1
            home = place([P, end - begin, PASS_BYTES], U8, f"w13_words{m}{begin}")
            rows = (w1_words, w3_words)[m].bitcast(I32).rearrange("e s p c -> p (e s) c")
            nc.sync.dma_start(home[:].bitcast(I32), rows[:, begin:end, :])
            for i in range(begin, end):
                w13_words[i // PASSES, m, i % PASSES] = home[:, i - begin, :]

        def load_scale_rows(plane, scales, planes, r):
            src = scales.bitcast(I32).rearrange("e s (q r) c -> r q (e s) c", r=4)
            dst = plane.bitcast(I32).rearrange("p (a c) -> p a c", a=planes)
            nc.sync.dma_start(dst[r:P:32, :, :], src[r])

        def load_scales(pair):
            for m in (W1, W3):
                for r in range(4):
                    scales = (w1_scales, w3_scales)[m][2 * pair : 2 * pair + 2]
                    load_scale_rows(w13_plane[pair, m][:], scales, 2 * PASSES, r)

        for m in (W1, W3):
            load_words(m, (0, 0), (0, 1))
        load_scales(0)
        for m in (W1, W3):
            load_words(m, (0, 2), (1, 2))
        load_words(W1, (2, 0), (2, 2))
        load_scales(1)
        for m, e in ((W3, 2), (W1, 3)):
            load_words(m, (e, 0), (e, 1))
            load_words(m, (e, 2), (e, 2))
        load_words(W3, (3, 0), (3, 0))
        last_words = []
        for side in range(2):
            home = place([P, PASSES - 1, H], U8, f"last_words{side}")
            rows = w3_words[E - 1, 1:].bitcast(I32).rearrange("s p c -> p s c")
            nc.sync.dma_start(home[:].bitcast(I32), rows[:, :, side * H // 4 : (side + 1) * H // 4])
            last_words.append(home)
        w2_t = place([P, E, 2 * N], U8, "w2_t")
        nc.sync.dma_start(w2_t[:].bitcast(I32), w2_words[:, 0].bitcast(I32).rearrange("e p c -> p e c"))
        for r in range(4):
            load_scale_rows(w2_plane[:], w2_scales, E, r)

        slot_words, slot_plane = {}, {}

        def gather(made, window, dtype, s, experts, on=None):
            entries = offsets[:, C * experts[0] // 16 : C * (experts[-1] + 1) // 16]
            home = place([P, len(experts) * C], dtype, f"slots{made is slot_words}{s}{experts[0]}", on)
            nc.vector.tensor_copy(home[:], window[s][:].indirect(entries))
            for i, e in enumerate(experts):
                made[s, e] = home[:, C * i : C * (i + 1)]

        for s in range(PASSES):
            grp = place([P, T, PACK], BF16, f"x_grp{s}")
            dst = grp[:].rearrange("p (c i) t -> p c t i", i=4)
            src = x_raw[s][:].rearrange("p t (c i) -> p c t i", i=4)
            cut = VECTOR_TOKENS[s] // 4
            if cut:
                nc.vector.tensor_copy(dst[:, :cut], src[:, :cut])
            nc.scalar.activation(dst[:, cut:], src[:, cut:], COPY)
            nc.vector.quantize_mx(
                out=x_words[s][:].bitcast(E4M3), scales=x_plane[s][:], in_=grp[:].rearrange("p c t -> p (c t)")
            )
            if s == 1:
                gather(slot_plane, x_plane, U8, 0, PAIRS[1], on="x_raw1")
            if s == 2:
                gather(slot_words, x_words, U32, 1, PAIRS[1], on="x_raw2")
            gather(slot_words, x_words, U32, s, PAIRS[0])
            gather(slot_plane, x_plane, U8, s, PAIRS[0])
            if s == 0:
                gather(slot_words, x_words, U32, 0, PAIRS[1])
        gather(slot_plane, x_plane, U8, 1, PAIRS[1], on="x_grp2")
        gather(slot_words, x_words, U32, PASSES - 1, (2,))
        gather(slot_plane, x_plane, U8, PASSES - 1, (2,))

        def one_pass(acc, e, m, s, first, words):
            width = words.shape[1] // 2
            at = H * (PASSES * (e % 2) + s) + first
            nc.tensor.matmul_mx(
                out=acc,
                lhsT=slot_words[s, e].bitcast(E4M3),
                lhsT_scale=slot_plane[s, e],
                rhs=words.bitcast(E2M1),
                rhs_scale=w13_plane[e // 2, m][:, at : at + width],
                start=(s == 0),
                stop=(s == PASSES - 1),
            )

        def in_pairs(acc):
            return acc.rearrange("p (q u d) -> p u q d", u=2, d=2)

        def product(e, m, number):
            acc = bank(number, [P, H], f"acc{e}{m}")
            for s in range(PASSES):
                one_pass(acc[:], e, m, s, 0, w13_words[e, m, s])
            return in_pairs(acc[:])

        def hidden(e, b):
            h = place([P, 2, P, 2], BF16, f"h{e}")
            nc.vector.tensor_tensor(h[:], b, gate[e][:], MULT)
            return h

        h_words, h_plane = {}, {}

        def turn(h, room):
            for u in range(2):
                nc.tensor.transpose(room[:, C * u : C * (u + 1)], h[:].bitcast(F32)[:, u, :, 0], ident[:])

        def interleave(room, grp):
            nc.scalar.copy(grp.bitcast(F32).rearrange("p (c u) -> p c u", u=2), room.rearrange("p (u c) -> p c u", u=2))

        def quantise(experts, grp):
            n = len(experts)
            words = place([P, n * C], U32, f"h_words{experts[0]}")
            plane = place([P, n * C], U8, f"h_plane{experts[0]}")
            nc.vector.quantize_mx(out=words[:].bitcast(E4M3), scales=plane[:], in_=grp)
            for i, e in enumerate(experts):
                h_words[e], h_plane[e] = words[:, C * i : C * (i + 1)], plane[:, C * i : C * (i + 1)]

        def hidden_half(h, e, side, acc):
            q = slice(side * P // 2, (side + 1) * P // 2)
            nc.vector.tensor_tensor(h[:, :, q, :], in_pairs(acc), gate[e][:, :, q, :], MULT)

        acc = {(e, m): bank(2 * m + e, [P, H], f"acc{e}{m}") for e in PAIRS[0] for m in (W1, W3)}
        order = [(0, m, s) for m in (W1, W3) for s in (0, 1)]
        order = order + [(1, W1, 0), (1, W1, 1), (0, W1, 2), (1, W1, 2), (0, W3, 2)] + [(1, W3, s) for s in range(PASSES)]
        for e, m, s in order:
            one_pass(acc[e, m][:], e, m, s, 0, w13_words[e, m, s])
        for e in PAIRS[0]:
            nc.scalar.activation(gate[e][:], in_pairs(acc[e, W1][:]), RELU)
        h0 = hidden(0, in_pairs(acc[0, W3][:]))
        h1 = hidden(1, in_pairs(acc[1, W3][:]))
        gather(slot_words, x_words, U32, PASSES - 1, (3,), on="gate0")
        gather(slot_plane, x_plane, U8, PASSES - 1, (3,), on="gate1")
        shared = [bank(side, [P, H], f"shared{side}") for side in range(2)]
        for s in range(PASSES):
            for side in range(2):
                words = w13_words[2, W1, s][:, side * H : (side + 1) * H]
                one_pass(shared[side][:, : H // 2], 2, W1, s, side * H // 2, words)
        for side, h in enumerate((h0, h1)):
            turn(h, shared[side][:, H // 2 :])
        for side in range(2):
            q = slice(side * P // 2, (side + 1) * P // 2)
            nc.scalar.activation(gate[2][:, :, q, :], in_pairs(shared[side][:, : H // 2]), RELU)
        pair_grp = place([P, 2, C * PACK], BF16, "pair_grp")
        for side in range(2):
            interleave(shared[side][:, H // 2 :], pair_grp[:, side, :])
        h2 = hidden(2, product(2, W3, 4))
        quantise(PAIRS[0], pair_grp[:].rearrange("p e c -> p (e c)"))
        last_a = product(3, W1, 2)
        for side in range(2):
            q = slice(side * P // 2, (side + 1) * P // 2)
            nc.scalar.activation(gate[3][:, :, q, :], last_a[:, :, q, :], RELU)
        last = [bank(5, [P, H], "last_low"), bank(3, [P, H], "last_high")]
        for side in range(2):
            one_pass(last[side][:, : H // 2], 3, W3, 0, side * H // 2, w13_words[3, W3, 0][:, side * H : (side + 1) * H])
        for side in range(2):
            for s in range(1, PASSES):
                one_pass(last[side][:, : H // 2], 3, W3, s, side * H // 2, last_words[side][:, s - 1, :])
        h3 = place([P, 2, P, 2], BF16, "h3")
        for side in range(2):
            hidden_half(h3, 3, side, last[side][:, : H // 2])
        for e, h, room in ((2, h2, last[0][:, H // 2 :]), (3, h3, bank(6, [P, 2 * C], "turned3")[:])):
            turn(h, room)
            grp = place([P, C * PACK], BF16, f"h_grp{e}")
            interleave(room, grp[:])
            quantise((e,), grp[:])

        def second_layer(experts, half, number, copy):
            y = bank(number, [P, len(experts), C], f"y{experts[0]}{half}")
            for i, e in enumerate(experts):
                first = N * e + P * half
                nc.tensor.matmul_mx(
                    out=y[:, i, :],
                    lhsT=w2_t[:, e, 2 * P * half : 2 * P * (half + 1)].bitcast(E2M1),
                    lhsT_scale=w2_plane[:, first : first + P],
                    rhs=h_words[e].bitcast(E4M3),
                    rhs_scale=h_plane[e],
                    start=True,
                    stop=True,
                )
            copy(o_sb[half][:, :, experts[0] : experts[-1] + 1, :], y[:].rearrange("p e (m u) -> p m e u", m=R))

        for experts, numbers in ((PAIRS[0], (7, 4)), ((2,), (0, 1)), ((3,), (2, 3))):
            for half, copy in ((1, nc.scalar.copy), (0, nc.vector.tensor_copy)):
                second_layer(experts, half, numbers[half], copy)
        for half in (1, 0):
            nc.sync.dma_start(out[P * half : P * (half + 1), :], o_sb[half][:].rearrange("p m e u -> p (m e u)"))
